import numpy as np, ml_dtypes
CORES = [25,29,65,69,153,157,193,197]
N = 8
import mx_ref
BF = ml_dtypes.bfloat16
def gentries(a):
    return np.ascontiguousarray(a.reshape(8, 16, -1).transpose(0, 2, 1)).reshape(8, -1)
def gtable(e):
    e = np.asarray(e); return np.ascontiguousarray(e.reshape(8, -1, 16).transpose(0, 2, 1)).reshape(128, -1).astype(np.int32)
def gcols(t, e):
    v = np.concatenate([t.reshape(8, 16, -1, 4), np.zeros((8, 16, 1, 4), BF)], axis=2)
    return np.ascontiguousarray(np.stack([v[g][:, e[g]] for g in range(8)])).reshape(128, -1)
def tile(rs):
    return np.stack(rs, axis=2).reshape(128, -1).astype(BF)
def pick(q, e):
    c = np.concatenate([q[0].reshape(128, -1, 4), np.zeros((128, 1, 4), np.uint8)], axis=1); s = np.concatenate([q[1], np.ones((16, 1), np.uint8)], axis=1)
    return (np.ascontiguousarray(c[:, e].reshape(128, -1)), np.ascontiguousarray(s[:, e]))
def join(*qs):
    return (np.concatenate([q[0] for q in qs], axis=1), np.concatenate([q[1] for q in qs], axis=1))
def put(q, e, v):
    c, s = q[0].reshape(128, -1, 4).copy(), q[1].copy(); c[:, e] = v[0].reshape(128, -1, 4); s[:, e] = v[1]
    return (c.reshape(128, -1), s)
def pk(c, s):
    return (np.ascontiguousarray(c), mx_ref.live(s))
def emit(q):
    return q[0], q[1]
def packed(v, rng):
    q = [mx_ref.quantize(np.ascontiguousarray(v[r])) for r in range(N)]
    return np.stack([a for a, b in q]), np.stack([mx_ref.plane(b, rng) for a, b in q])
def values_of_codes():
    e, c = np.zeros((128, 128, 4), np.float32), np.zeros((128, 2, 4), np.uint8)
    e[np.arange(128), np.arange(128), 0] = 1
    c[:127, :, 0] = np.arange(256).reshape(2, 128).T[:127]
    return mx_ref.matmul(mx_ref.quantize(e.reshape(128, 512).astype(BF)), (c.reshape(128, 8), np.full((16, 2), 127, np.uint8))).T.reshape(-1).astype(np.float64)
CODE_VALUE, SCALE_VALUE = values_of_codes(), 2.0 ** (np.arange(256) - 127.0)
def decode(q):
    return (CODE_VALUE[q[0]].reshape(16, 8, -1, 4) * SCALE_VALUE[q[1]][:, None, :, None] + 0.0).reshape(128, -1).astype(np.float32)
def f(rng, *shape):
    return mx_ref.flush((rng.standard_normal(shape, dtype=np.float32) * np.exp2(rng.integers(-2, 3, shape[:-1] + (1,)))).astype(BF))
def wide(rng, *shape, cols=0):
    v = rng.standard_normal(shape, dtype=np.float32) * np.exp2(rng.integers(-12, 13, shape)).astype(np.float32)
    if cols: v *= np.repeat(np.exp2(rng.integers(-cols, cols + 1, shape[:-2] + (1, shape[-1] // 4))) * (rng.random(shape[:-2] + (1, shape[-1] // 4)) > 0.0625), 4, axis=-1).astype(np.float32)
    return mx_ref.flush(v.astype(BF))
C, K, M, R = 384, 32, 12, 3
BASE = M * np.concatenate([np.arange(K), np.arange(K)])
def matrices(a):
    return a.reshape(8, 16, K // 16, M, M).transpose(0, 2, 1, 3, 4).reshape(8, K, M, M).astype(np.int64)
def stored(m):
    return np.ascontiguousarray(m.reshape(8, K // 16, 16, M, M).transpose(0, 2, 1, 3, 4)).reshape(128, -1)
def numbers_of(rng):
    return {"x": np.array(f(rng, N, 128, 4 * C)), "u": np.array(f(rng, N, 128, 512)), "v": np.array(f(rng, N, 128, 512))}
def nodes(rng):
    return np.stack([gtable(np.stack([rng.permutation(C) for g in range(8)])) for r in range(N)])
def arrows(a):
    a = np.triu(a, 1)
    a = a - a.swapaxes(-1, -2)
    return np.stack([stored(a[r]) for r in range(N)]).astype(np.int32)
def some_arrows(rng):
    return rng.integers(-3, 4, (N, 8, K, M, M)) * (rng.random((N, 8, K, M, M)) < 0.6)
def laid(w, nd):
    w = w.reshape(N, 8, 16, C, 4)
    t = np.zeros_like(w)
    for r in range(N):
        e = gentries(nd[r])
        for g in range(8): t[r, g][:, e[g]] = w[r, g]
    return t.reshape(N, 128, 4 * C).astype(BF)
def weights(rng, still=[], by=1.0):
    w = np.array(f(rng, N, 128, 2048)).reshape(N, 8, 16, 4, 8, 16, 4)
    for i in still:
        w[:, :, i] = 0
        w[:, :, :, :, :, i] = 0
    w = mx_ref.flush((w.astype(np.float32) * np.float32(by)).astype(BF))
    c, s = packed(np.ascontiguousarray(w).reshape(N, 128, 2048), rng)
    return {"wc": c, "ws": s}
def setup_inputs(rng):
    return {**numbers_of(rng), "nd": nodes(rng), "ar": arrows(some_arrows(rng)), **weights(rng)}
def setup_inputs_ties(rng):
    d = numbers_of(rng)
    nd = nodes(rng)
    w = d["x"].reshape(N, 8, 16, C, 4)
    w[:, :, 0] = 0
    w[:, :, 0, :, 0] = rng.integers(1, 4, (N, 8, C)).astype(np.float32).astype(BF)
    u = d["u"].reshape(N, 128, 128, 4)
    u[:, :, ::16] = 0
    o = rng.permutation(N)
    for r in range(N):
        for h in range(0, 128, 16): u[r, h, h, 0] = 0.0 if r == o[0] else -1.0 if r == o[1] else 1.0
    return {"x": laid(w, nd), "u": u.reshape(N, 128, 512), "v": d["v"], "nd": nd, "ar": arrows(some_arrows(rng)), **weights(rng, [0])}
def setup_inputs_near(rng):
    d = numbers_of(rng)
    nd = nodes(rng)
    w = d["x"].astype(np.float32).reshape(N, 8, 16, K, M, 4)
    w[:, :, 0] = 0
    w[:, :, 8:] = 0
    s = rng.integers(0, 16, (N, 8, K, M))
    w[:, :, 8] = ((s[..., None] >> np.arange(4)) & 1) * np.exp2(np.arange(4) - 23.0)
    u = d["u"].reshape(N, 128, 128, 4)
    u[:, :, ::16] = 0
    o = rng.permutation(N) % 4
    for r in range(N):
        k = 1.0 if o[r] == 0 else 2.0 ** -30
        c = rng.choice([-1.0, 1.0], (8, K, 1))
        if o[r] < 2:
            w[r, :, 0, :, :, 0] = c
            w[r, :, 11, :, :, 0] = 2.0 ** -10
        elif o[r] == 2:
            far = np.argsort(rng.random((8, K, M)), axis=2)
            w[r, :, 0, :, :, 0] = 1.0 * (far == 0) - 1.0 * (far == 1)
            for g in rng.permutation(8)[:4]: w[r, g, 0, rng.integers(K), rng.integers(M), 0] = 2.0 ** 26
        else:
            w[r, :, 8] = 0
            w[r, :, 8, :, :, 0] = c * rng.integers(8, 16, (8, K, M)) * 2.0 ** -27
        for h in range(0, 128, 16):
            if o[r] < 2:
                u[r, h, h, 0] = k
                u[r, h + 11, h, 0] = k
            if o[r] == 2: u[r, h, h, 0] = 16.0
            if o[r] < 3: u[r, h + 8, h] = k
            else: u[r, h + 8, h, 0] = k
    return {"x": laid(w, nd), "u": u.reshape(N, 128, 512), "v": d["v"], "nd": nd, "ar": arrows(some_arrows(rng)), **weights(rng, [0, 8, 9, 10, 11, 12, 13, 14, 15])}
def setup_inputs_huge(rng):
    d = numbers_of(rng)
    o = rng.permutation(N)
    a = some_arrows(rng)
    x = 0.8 + 0.1 * rng.random((N, 128, C, 4))
    u = d["u"].reshape(N, 128, 128, 4)
    for r in range(N):
        c = rng.choice([-1.0, 1.0], (C, 1))
        k = 2.0 ** 30 * (1.0 - 0.1 * rng.random((128, 8, 4)))
        if o[r] < 2: c = -np.ones((C, 1))
        if o[r] == 3:
            c = -np.ones((C, 1))
            c[rng.permutation(C)[:K]] = 1.0
            x[r] = 0.9375
            k[:] = 2.0 ** 30
        if o[r] % 2 == 1: a[r] = 0
        x[r] *= c * (2.0 ** 30 if o[r] % 2 == 1 else 2.0 ** 28 if o[r] == 0 else 2.0 ** 27)
        u[r, :, ::16] = k.astype(np.float32).astype(BF)
    return {"x": x.astype(np.float32).reshape(N, 128, 4 * C).astype(BF), "u": u.reshape(N, 128, 512), "v": d["v"], "nd": nodes(rng), "ar": arrows(a), **weights(rng, [], 2.0 ** -14)}
def setup_inputs_knots(rng):
    d = numbers_of(rng)
    e = rng.permutation(N)
    kind = rng.integers(0, 4, (N, 8, K, 1, 1))
    kind[e[0]] = 0
    kind[e[1]] = 1
    sign = rng.choice([-1, 1], (N, 8, K, M, M))
    half = sign * (rng.random((N, 8, K, M, M)) < 0.5)
    a = np.where(kind == 0, 0, np.where(kind == 1, sign * rng.integers(1, 4, (N, 8, K, M, M)), np.where(kind == 2, half, 3 * half)))
    place = np.arange(8)[:, None, None] * 4 + np.arange(4)
    most = place == rng.integers(0, 32, (N, 16, 1, C, 1))
    x = (129.0 + 2.0 * rng.integers(0, 64, (N, 16, 8, C, 4))) * np.exp2(-7.0 - rng.integers(8, 15, (N, 16, 8, C, 4)))
    x = np.where(most, 1.96875, x) * rng.choice([-1.0, 1.0], (N, 16, 8, C, 4)) * np.exp2(rng.integers(-2, 3, (N, 16, 1, C, 1)))
    return {"x": x.astype(np.float32).reshape(N, 128, 4 * C).astype(BF), "u": d["u"], "v": d["v"], "nd": nodes(rng), "ar": arrows(a), **weights(rng)}
def setup_inputs_spread(rng):
    d = setup_inputs(rng)
    d["x"] = wide(rng, N, 128, 4 * C, cols=6)
    return d
def check_inputs(d):
    b = []
    for k in ("x", "u", "v"):
        a = np.abs(d[k].astype(np.float32))
        if not (np.isfinite(a).all() and ((a == 0) | (a >= 2.0 ** -30) & (a <= 2.0 ** 30)).all()): b.append("a value of " + k)
    none, least, most = [emit(mx_ref.quantize(np.full((128, 16), k, np.float32).astype(BF)))[1][0, 0] for k in (0.0, 2.0 ** -30, 2.0 ** 30)]
    for r in range(N):
        if (np.sort(gentries(d["nd"][r]), axis=1) != np.arange(C)).any(): b.append("nd: a group without every column once")
        a = matrices(d["ar"][r])
        if (np.abs(a) > 3).any(): b.append("an entry of ar")
        if (a != -a.swapaxes(-1, -2)).any(): b.append("ar: B[j, i] isn't -B[i, j]")
        if ((d["wc"][r] & 0x7F) == 0x7F).any(): b.append("wc: a code that is no number")
        s = mx_ref.live(d["ws"][r])
        if ((s != none) & ((s < least) | (s > most))).any(): b.append("ws: a scale out of range")
    return b
def parts(t, n, e):
    return gcols(t, np.where(e < 0, -1, np.take_along_axis(n, BASE + np.maximum(e, 0), axis=1))).astype(np.float32)
def pair(t, n, w):
    e = np.argsort(-w, axis=2, kind="stable")[:, :, :2]
    e = np.where(np.take_along_axis(w, e, axis=2) > 0, e, -1)
    return ((parts(t, n, e[:, :, 0]) + parts(t, n, e[:, :, 1])) * np.float32(0.5)).astype(BF).astype(np.float32)
def reference(x, u, v, nd, ar, wc, ws):
    qu = [mx_ref.quantize(u[r]) for r in range(N)]
    lay = [pk(wc[r], ws[r]) for r in range(N)]
    now = [x[r] for r in range(N)]
    node = [gentries(nd[r]) for r in range(N)]
    arrow = [matrices(ar[r]) for r in range(N)]
    for t in range(R):
        held, made, sent, into = [], [], [], []
        for r in range(N):
            q = mx_ref.quantize(now[r])
            own = decode(q).astype(BF)
            s = mx_ref.matmul(qu[r], q)[::16] + np.float32(0.0)
            s = np.take_along_axis(s, node[r], axis=1).reshape(8, K, M)
            first = np.argmax(s, axis=2)
            row = np.take_along_axis(arrow[r], first[:, :, None, None], axis=2)[:, :, 0]
            free = (row == 0) & (np.arange(M) != first[:, :, None])
            second = np.argmax(np.where(free, s, -np.inf), axis=2)
            k = np.concatenate([first, second], axis=1)
            full = np.concatenate([np.ones((8, K), bool), free.any(axis=2)], axis=1)
            row = np.concatenate([row, np.take_along_axis(arrow[r], second[:, :, None, None], axis=2)[:, :, 0]], axis=1) * full[:, :, None]
            y = (np.maximum(pair(own, node[r], -row), pair(own, node[r], row)) - parts(own, node[r], np.where(full, k, -1))).astype(BF)
            held.append(own)
            made.append(y)
            sent.append(mx_ref.quantize(y))
            e = np.tile(np.arange(C), (8, 1))
            g, i = np.nonzero(full)
            e[g, np.take_along_axis(node[r], BASE + k, axis=1)[g, i]] = C + i
            into.append(e)
            more = (np.abs(row)[:, :, :, None] * row[:, :, None, :] - row[:, :, :, None] * np.abs(row)[:, :, None, :]) // 2
            turn = np.ones((8, 2 * K, M), np.int64)
            np.put_along_axis(turn, k[:, :, None], np.where(full, -1, 1)[:, :, None], axis=2)
            turn = turn[:, :K] * turn[:, K:]
            arrow[r] = np.clip(arrow[r] + more[:, :K] + more[:, K:], -3, 3) * turn[:, :, :, None] * turn[:, :, None, :]
        for r in range(N):
            q = sent[(r - 1) % N]
            new = tile([mx_ref.matmul(pick(lay[r], np.arange(128 * b, 128 * b + 128)), q) * np.float32(0.03125) + made[r][:, b::4].astype(np.float32) for b in range(4)])
            now[r] = gcols(np.concatenate([held[r], new], axis=1), into[r])
    y, oa = np.zeros((N, 128, C), np.float32), np.zeros(ar.shape, np.float32)
    oc, osc = np.zeros((N, 128, 4 * C), np.uint8), np.zeros((N, 16, C), np.uint8)
    for r in range(N):
        q = mx_ref.quantize(now[r])
        y[r] = mx_ref.matmul(mx_ref.quantize(v[r]), q)
        oa[r] = stored(arrow[r])
        oc[r], osc[r] = emit(q)
    return {"y": y, "oa": oa, "oc": oc, "osc": osc}

@@ -1,0 +1,518 @@
+from concourse.mybir import dt, AluOpType, ActivationFunctionType
+
+N, C, R = 8, 384, 3
+BIG = 2.0 ** 90
+PEN, NONE = 2.0 ** 80, 2.0 ** 79
+Q = 8192.0
+CW = 416
+WAKE, NEAR, FAR = 120.0, 3000.0, 6200.0
+SCRATCH, CODES = {}, set()
+
+
+def declare(dtype, spec):
+    for item in spec.split():
+        name, cols = item.split(":")
+        where = "psum" if name in ("psP", "psE") else "sbuf"
+        SCRATCH[name] = (where, [128, int(cols)], dtype)
+        if dtype == "float8_e4m3fn_x4":
+            CODES.add(name)
+
+
+declare("bfloat16", "fx:1664 fh:1664 ut:512 vt0:512 yt:512 zt:512 et:520 ones:128 ga:512 sa:768 sb:768 sy:768 y32:256 vt:256 "
+        "h1:364 h2:364 pw:144 w:104 pp:52 nn:52 oo:52 ei:576 pr:576 s5:576 sp:144 iC:384 cap:384 we:182 rs2:384 sg:576")
+declare("float8_e4m3fn_x4", "uq:128 urq:128 vq:128 eq:512 zq:128 wq:512 xq:384 " + " ".join("yc%d:128 lc%d:128 rc%d:64" % (t, t, t) for t in range(R)))
+declare("uint8", "us:128 urs:128 vs:128 es:512 zs:128 wp:512 xs:384 " + " ".join("yp%d:128 lp%d:128 rp%d:64" % (t, t, t) for t in range(R)))
+declare("float32", "psP:1536 psE:2048 vf:256 psc:384 gm:384 sc:384 pm1:24 ix:4 junk:64 s2:364 pm2:26 kk:728 ka:104 pmb:105 mn:104 sm:104 "
+        "bt:368 pen:368 win1:344 win2:344 tb1:368 tp0:368 ob:288 ysb:384 rt:384 iK:384 nlf:24 pf:4 pd:8 it13:13 k2i:24 k2c:52 "
+        "rsx:160 lm:46 lA:46 lB:46 lC:46 lD:46 lE:46 lF:46 lG:46 lH:46 lI:46 uA:36 uX:36 uY:36 uZ:36 uB:36 uC:36")
+declare("int32", "di:16 dj:16 ndi:24 ari:288 pI:4 pA:4 ui:8 li:46")
+declare("uint16", "oL:20 so:16 nd16:24 nl:24 ul:8 L:156")
+PART = {"oA": ("oL", 0, 8), "oB": ("oL", 8, 8), "oK": ("oL", 16, 4), "rs24": ("rsx", 0, 24), "rs26": ("rsx", 24, 26), "rsk": ("rsx", 52, 104),
+        "LI": ("L", 48, 36), "LJ": ("L", 84, 36), "L4": ("L", 120, 36)}
+DMAS = 26
+SEMAPHORES = ["qv", "qs", "qt", "qg", "sent"] + ["d%d" % i for i in range(DMAS)] + ["ac%d" % t for t in range(R)] + ["ap%d" % t for t in range(R)]
+
+
+def route(T, topo, r):
+    src, dst = T.cores[r], T.cores[(r + 1) % N]
+    if topo.may_write(src, dst):
+        return src, dst, None, None
+    c = [k for k in topo.cores_of(src) if k not in T.cores and topo.may_write(k, dst)]
+    c.sort(key=lambda k: (topo.die(k) != topo.die(src), k))
+    return src, dst, c[0], c[1 % len(c)]
+
+
+def u8(T, name, a, b):
+    v = T[name][:, a:b]
+    return v.bitcast(dt.uint8) if name in CODES else v
+
+
+def send(g, T, topo, core, to, out, src, sem):
+    rid, pid = topo.addr(to, core)
+    g.remote_dma(u8(T, out, 0, 64), u8(T, src, 0, 64), T.sem[sem], T.sem.sent, pid, rid, topo.mask(core, to))
+    return len(topo.engines(core, to))
+
+
+def relay_program(g, core, T, topo):
+    total = 0
+    for t in range(R):
+        for r in range(N):
+            src, dst, ca, cb = route(T, topo, r)
+            for k, sem, mid, out in ((ca, "ac%d" % t, "rc%d" % t, "lc%d" % t), (cb, "ap%d" % t, "rp%d" % t, "lp%d" % t)):
+                if k == core:
+                    g.wait_ge(T.sem[sem], len(topo.engines(src, core)))
+                    total += send(g, T, topo, core, dst, out, mid, sem)
+    if total:
+        g.wait_ge(T.sem.sent, total)
+
+
+def overlap(a, b):
+    if a[0] != b[0] or a[1] >= b[2] or b[1] >= a[2]:
+        return False
+    return not (a[3] == b[3] > 1 and (a[1] - b[1]) % a[3])
+
+
+def rank_program(g, core, T, topo):
+    rank = T.rank_of(core)
+    if rank is None:
+        relay_program(g, core, T, topo)
+        return
+    A = AluOpType
+    F = ActivationFunctionType
+    queue = {"v": g.vector, "s": g.scalar, "t": g.tensor, "g": g, "y": g.sync}
+    count = {}
+    known = {k: {} for k in queue}
+    direct = route(T, topo, (rank - 1) % N)[2] is None
+    free = ["d%d" % i for i in range(DMAS)]
+    ops, last = [], {}
+
+    def add(q, call, reads, writes, cost, sem=None, inc=1, after=(), arrivals=(), lag=0.0):
+        k = len(ops)
+        deps = {d: lag for d in after}
+        for kind, regions in (("r", reads), ("w", writes)):
+            for x in regions:
+                for o, y, d in last.get(x[0], []):
+                    if (kind == "w" or o == "w") and overlap(x, y):
+                        deps.setdefault(d, 0.0)
+        for x in writes:
+            last[x[0]] = [e for e in last.get(x[0], []) if not (e[1][1] >= x[1] and e[1][2] <= x[2] and x[3] == 1)]
+        for kind, regions in (("r", reads), ("w", writes)):
+            for x in regions:
+                last.setdefault(x[0], []).append((kind, x, k))
+        ops.append((q, call, cost, sem or "q" + q, inc, deps, arrivals))
+        return k
+
+    def run(q, call, reads, writes, cost, arr=None):
+        reads = [x for o in reads for x in o[1]]
+        writes = [x for o in writes for x in o[1]]
+        both = [x for x in reads if x[0] in ("psP", "psE")]
+        add(q, lambda e: call(e).then_inc(T.sem["q" + q], 1), [x for x in reads if x not in both], writes + both, cost,
+            after=[arr[0]] if arr else (), arrivals=arr[1] if arr else (), lag=(NEAR if direct else FAR) if arr else 0.0)
+
+    def dma(q, out, in_, reads, writes):
+        sem = free.pop(0)
+        add(q, lambda e: e.dma_start(out, in_).then_inc(T.sem[sem], 16), reads, writes, 2700.0, sem, 16)
+
+    def post(writes):
+        def call(e):
+            for to, out, mine, sem in writes:
+                count["sent"] = count.get("sent", 0) + send(e, T, topo, core, to, out, mine, sem)
+        return add("g", call, [(w[2], 0, 128, 1) for w in writes], [], 1400.0, "sent", 0)
+
+    def issue():
+        n = len(ops)
+        users = [[] for _ in range(n)]
+        far = [0.0] * n
+        for k in range(n):
+            for d in ops[k][5]:
+                users[d].append(k)
+        for k in range(n - 1, -1, -1):
+            far[k] = ops[k][2] + max([far[u] + WAKE + ops[u][5][k] for u in users[k]] or [0.0])
+        line = {q: [] for q in queue}
+        start = [0.0] * n
+        for k in sorted(range(n), key=lambda k: (-far[k], k)):
+            q, cost, deps = ops[k][0], ops[k][2], ops[k][5]
+            t0 = max([start[d] + ops[d][2] + WAKE + deps[d] for d in deps] or [0.0])
+            busy = 60.0 if ops[k][4] == 16 else cost
+            at = 0
+            for a, b in line[q]:
+                if t0 + busy <= a:
+                    break
+                t0 = max(t0, b)
+                at += 1
+            line[q].insert(at, (t0, t0 + busy))
+            start[k] = t0
+        mark = [None] * n
+        for k in sorted(range(n), key=lambda k: (start[k], -far[k], k)):
+            q, call, cost, sem, inc, deps, arrivals = ops[k]
+            for d in sorted(deps, key=lambda d: -mark[d][1]):
+                if mark[d][0] != "sent":
+                    need(q, *mark[d])
+            for a, v in arrivals:
+                need(q, a, v, {})
+                count[a] = v
+            call(queue[q])
+            if inc:
+                count[sem] = count.get(sem, 0) + inc
+            mark[k] = (sem, count.get(sem, 0), dict(known[q]))
+
+    def need(q, sem, val, clock):
+        if known[q].get(sem, 0) < val:
+            queue[q].wait_ge(T.sem[sem], val)
+            known[q][sem] = val
+            for s in clock:
+                known[q][s] = max(known[q].get(s, 0), clock[s])
+
+    def V(name, a=0, b=None, step=1):
+        name, o, n = PART.get(name, (name, 0, None))
+        b = (SCRATCH[name][1][1] if n is None else n) if b is None else b
+        a, b = a + o, b + o
+        return (T[name][:, a:b:step] if step > 1 else T[name][:, a:b], [(name, a, b, step)])
+
+    def ind(win, off):
+        return (win[0].indirect(off[0]), win[1] + off[1], True)
+
+    def val(s):
+        return s[0] if isinstance(s, tuple) else s
+
+    def reg(*ss):
+        return [s for s in ss if isinstance(s, tuple)]
+
+    def size(v):
+        name, a, b, step = v[1][0]
+        return (b - a + step - 1) // step
+
+    def fast(n, *v):
+        return max(64, n * (0.5 if all(SCRATCH[x[1][0][0]][2] in ("bfloat16", "uint16") for x in v) else 1))
+
+    def tt(out, a, b, op):
+        n = size(out)
+        cost = 50 + 1.6 * n if len(a) > 2 else max(64, n if a[1][0][0] in ("psP", "psE") else 2 * n)
+        run("v", lambda e: e.tensor_tensor(out[0], a[0], b[0], op), [a, b], [out], cost)
+
+    def ts(out, a, s1, op0, s2=None, op1=None):
+        if op1 is None:
+            run("v", lambda e: e.tensor_scalar(out[0], a[0], val(s1), None, op0), [a] + reg(s1), [out], fast(size(out), a, out))
+        else:
+            run("v", lambda e: e.tensor_scalar(out[0], a[0], val(s1), val(s2), op0, op1), [a] + reg(s1, s2), [out], fast(size(out), a, out))
+
+    def cp(out, a):
+        run("v", lambda e: e.tensor_copy(out[0], a[0]), [a], [out], fast(size(out), a, out))
+
+    def scan(out, d0, d1, initial, op0, op1):
+        run("v", lambda e: e.tensor_tensor_scan(out[0], d0[0], d1[0], initial, op0, op1), [d0, d1], [out], fast(size(out), d0, d1, out))
+
+    def fill(out, c):
+        run("v", lambda e: e.memset(out[0], c), [], [out], max(64, size(out)))
+
+    def quant(q, s, t):
+        run("v", lambda e: e.quantize_mx(q[0], s[0], t[0]), [t], [q, s], 15 + 0.26 * size(t))
+
+    def mm(out, w, ws, x, xs, arr=None):
+        run("t", lambda e: e.matmul_mx(out[0], w[0], ws[0], x[0], xs[0], True, True), [w, ws, x, xs], [out], 1.7 * size(x) + 18, arr)
+
+    def act(out, a, scale=1.0, func=None, bias=None, accum=None):
+        kw = {}
+        if scale != 1.0:
+            kw["scale"] = scale
+        if bias is not None:
+            kw["bias"] = val(bias)
+            func = func or F.Identity
+        if accum is not None:
+            kw["accum_out"] = accum[0]
+        run("s", lambda e: e.activation(out[0], a[0], func or F.Copy, **kw), [a] + reg(bias), [out] + reg(accum),
+            70 + 1.6 * size(out) if len(a) > 2 else max(64, size(out)) + (20 if accum is not None else 0))
+
+    def iota(out, pattern, base=0, cm=0):
+        cost = 150 + 2 * size(out)
+        if SCRATCH[out[1][0][0]][2] == "int32":
+            run("g", lambda e: e.iota(out[0], pattern, base, cm), [], [out], cost)
+        else:
+            run("g", lambda e: e.iota(out[0], pattern, base, cm, allow_small_or_imprecise_dtypes=True), [], [out], cost)
+
+    def select(out, pattern, fill_, base):
+        run("g", lambda e: e.affine_select(out[0], out[0], pattern, A.not_equal, fill_, base, 0), [out], [out], 200 + 2 * size(out))
+
+    dma("y", T.ndi[:], T.nd[:], [], V("ndi")[1])
+    dma("s", T.ut[:], T.u[:], [], V("ut")[1])
+    dma("y", T.fx[:, 0:768], T.x[:, 0:768], [], V("fx", 0, 768)[1])
+    dma("s", T.fx[:, 768:1536], T.x[:, 768:1536], [], V("fx", 768, 1536)[1])
+    dma("y", T.ari[:], T.ar[:], [], V("ari")[1])
+    dma("y", T.wq[:, 0:512].bitcast(dt.uint8), T.wc[:], [], V("wq")[1])
+    dma("y", T.wp[:], T.ws[:], [], V("wp")[1])
+    dma("y", T.vt0[:], T.v[:], [], V("vt0")[1])
+
+    lm = lambda n, a=0, b=46: V(n, a, b)
+    iota(V("pI"), [[0, 4]], 0, 1)
+    iota(lm("lm"), [[0, 2], [16, 23]])
+    iota(V("uA"), [[0, 2], [1, 6], [4, 3]], 1)
+    iota(V("uZ"), [[144, 2], [0, 6], [48, 3]])
+    iota(V("iK"), [[1, 384]])
+    iota(V("iC"), [[0, 24], [1, 16]])
+    iota(V("ui"), [[16, 8]])
+    iota(V("ones"), [[0, 128]], 1)
+    iota(V("et"), [[0, 520]])
+    run("g", lambda e: e.affine_select(T.et[:, 3:515:4], T.ones[:], [[-1, 128]], A.is_equal, 0.0, 0, 1), [V("ones")], [V("et")], 460.0)
+    iota(V("k2i"), [[0, 2], [-512, 12]], -512)
+    for n in ("win1", "win2"):
+        iota(V(n, 288, 344), [[0, 56]])
+    act(V("rsx"), V("iC", 0, 160), 0.0, bias=BIG)
+    for k, c in ((1, PEN), (39, NONE), (53, NONE)):
+        select(V("win2", 288, 344), [[1, 56]], c, -k)
+    select(V("rs24"), [[0, 2], [1, 12]], -BIG, 0)
+    select(V("rs26"), [[0, 2], [1, 13]], -BIG, 0)
+    iota(V("we"), [[0, 13], [1, 14]])
+    iota(V("k2c"), [[0, 52]], -8192)
+    select(V("rsk"), [[0, 8], [1, 13]], -BIG, -12)
+    for b in range(4):
+        iota(V("fh", CW * b + 384, CW * b + CW), [[0, 32]])
+    iota(V("yt", 256, 512), [[0, 256]])
+    iota(V("uX"), [[13, 2], [0, 18]])
+    iota(V("uY"), [[13, 2], [0, 6], [4, 3]])
+    iota(V("it13"), [[1, 13]])
+    iota(V("sb", 0, 768, 3), [[0, 256]])
+    act(V("sa", 2, 768, 3), V("iC", 0, 256), 0.0, bias=-BIG)
+    act(V("sb", 2, 768, 3), V("iC", 0, 256), 0.0, bias=BIG)
+    iota(V("zt"), [[0, 512]])
+
+    ts(V("pA", 0, 1), V("pI", 0, 1), 15, A.bitwise_and)
+    ts(V("pA", 1, 2), V("pI", 1, 2), 2, A.logical_shift_right, 3, A.bitwise_and)
+    ts(V("pA", 2, 3), V("pI", 2, 3), 3, A.bitwise_and)
+    ts(V("pA", 3, 4), V("pI", 3, 4), 1, A.bitwise_and)
+    cp(V("pf"), V("pA"))
+    p16, p4, pt, p1 = (V("pf", k, k + 1) for k in range(4))
+    act(V("pd", 2, 3), p16, -1.0, bias=182.0)
+    act(V("pd", 5, 6), p4, 12.0)
+    act(V("uB"), V("uA"), bias=p4)
+    ts(lm("lB"), lm("lm"), V("pd", 2, 3), A.is_ge)
+    ts(lm("lC"), lm("lB"), -182.0, A.mult, p16, A.add)
+    ts(V("uC"), V("uB"), 12.0, A.is_ge, -12.0, A.mult)
+    tt(lm("lD"), lm("lC"), lm("lm"), A.add)
+    tt(V("uC"), V("uC"), V("uB"), A.add)
+    ts(lm("li"), lm("lD"), 1.0 / 14, A.mult, -6.5 / 14, A.add)
+    act(V("pmb", 0, 1), p16, 0.0, bias=-BIG)
+    cp(lm("lE"), lm("li"))
+    tt(V("uZ"), V("uZ"), V("uC"), A.add)
+    ts(lm("lC"), lm("lE"), -14.0, A.mult)
+    ts(V("L4"), V("uZ"), V("pd", 5, 6), A.add)
+    tt(lm("lF"), lm("lC"), lm("lD"), A.add)
+    ts(lm("lF", 23, 46), lm("lF", 23, 46), 1.0, A.add)
+    tt(lm("lC"), lm("lF"), lm("lE"), A.subtract)
+    act(lm("lI"), lm("lB"), 72.0)
+    ts(lm("lD"), lm("lC"), 0.0, A.is_lt, 12.0, A.mult)
+    tt(lm("lC"), lm("lC"), lm("lD"), A.add)
+
+    def score_products(w, ws):
+        for k in range(3):
+            a = 128 * k
+            quant(V("xq", a, a + 128), V("xs", a, a + 128), V("fx", 4 * a, 4 * a + 512))
+            mm(V("psP", 512 * k, 512 * k + 128), w, ws, V("xq", a, a + 128), V("xs", a, a + 128))
+
+    def unpack_products():
+        for b in range(4):
+            mm(V("psE", 512 * b, 512 * b + 384), V("eq", 128 * b, 128 * b + 128), V("es", 128 * b, 128 * b + 128), V("xq"), V("xs"))
+
+    cp(V("nd16"), V("ndi"))
+    act(V("rt"), ind(V("iK"), V("nd16")))
+    for x in range(2):
+        dma("y", T.nlf[:, 12 * x:12 * x + 12], T.rt[0:128:16, 192 * x:192 * x + 192], V("rt")[1], V("nlf", 12 * x, 12 * x + 12)[1])
+    act(V("cap"), V("iC"), -1.0, F.Square, p16)
+    act(V("cap"), V("cap"), -2.0 * BIG, bias=BIG)
+    act(V("rs2"), V("iC"), 0.0, bias=BIG)
+    cp(V("ul"), V("ui"))
+    fill(V("rs2", 0, 384, 16), -BIG)
+    quant(V("uq"), V("us"), V("ut"))
+    run("v", lambda e: e.tensor_copy(T.urq[:, 0:128].bitcast(dt.uint32), T.uq[:, 0:128].bitcast(dt.uint32).indirect(T.ul[:, 0:8])),
+        [V("uq"), V("ul")], [V("urq")], 250.0)
+    act(V("urs"), ind(V("us"), V("ul")))
+    score_products(V("urq"), V("urs"))
+    act(V("ei"), ind(V("ari"), V("L4")))
+    act(V("pw"), V("ei", 0, 576, 4))
+    cp(V("nl"), V("nlf"))
+    act(lm("lG"), lm("lC"), 12.0, bias=-12.0)
+    act(lm("lD"), lm("lC"), -12.0, bias=276.0)
+    ts(lm("lH"), lm("lC"), 7.0, A.is_ge, 1000.0, A.mult)
+    tt(lm("lG"), lm("lG"), lm("lE"), A.add)
+    tt(lm("lD"), lm("lD"), lm("lF"), A.add)
+    tt(lm("lG"), lm("lG"), lm("lH"), A.add)
+    ts(lm("lH"), lm("lC"), 0.0, A.is_equal, 289.0, A.mult)
+    tt(lm("lG"), lm("lG"), lm("lD"), A.min)
+    tt(lm("lG"), lm("lG"), lm("lI"), A.add)
+    tt(lm("lG"), lm("lG"), lm("lH"), A.max)
+    e0, e1 = lm("lF", 0, 23), lm("lF", 23, 46)
+    act(lm("lA"), lm("lB"), 14.0, bias=314.0)
+    act(lm("lC", 0, 23), lm("lB", 0, 23), 12.0, bias=290.0)
+    ts(lm("lH"), lm("lF"), 12.0, A.is_ge, 288.0, A.mult)
+    ts(lm("lI"), lm("lE"), 12.0, A.is_equal)
+    tt(lm("lG"), lm("lG"), lm("lH"), A.max)
+    tt(lm("lA"), lm("lA"), lm("lF"), A.add)
+    tt(lm("lC", 0, 23), lm("lC", 0, 23), lm("lE", 0, 23), A.add)
+    ts(lm("lD", 0, 23), e0, 13.0, A.is_equal)
+    ts(lm("lD", 23, 46), e1, 13.0, A.is_lt)
+    tt(lm("lA"), lm("lA"), lm("lI"), A.mult)
+    tt(lm("lC", 0, 23), lm("lC", 0, 23), lm("lD", 0, 23), A.mult)
+    tt(lm("lA", 23, 46), lm("lA", 23, 46), lm("lD", 23, 46), A.mult)
+    tt(lm("lG", 0, 23), lm("lG", 0, 23), lm("lC", 0, 23), A.max)
+    tt(lm("lG"), lm("lG"), lm("lA"), A.max)
+    cp(V("L", 0, 23), lm("lG", 0, 23))
+    cp(V("L", 24, 47), lm("lG", 23, 46))
+    L0, L1 = V("L", 0, 23), V("L", 24, 47)
+
+    def penalties():
+        act(V("win2", 0, 144), V("pw"), PEN, F.Abs)
+        act(V("win2", 144, 288), V("pw"), PEN, F.Abs)
+        act(V("tp0"), ind(V("win2"), L0))
+
+    def weights():
+        act(V("win1", 0, 144), V("pw"), Q)
+        act(V("win1", 144, 288), V("pw"), -Q)
+        act(V("tb1"), ind(V("win1"), L1))
+
+    def table_p():
+        tt(V("pen"), ind(V("win2"), L1), V("tp0"), A.subtract)
+
+    def table_b():
+        tt(V("bt"), ind(V("win1"), L0), V("tb1"), A.subtract)
+
+    for t in range(R):
+        if t:
+            score_products(V("urq"), V("urs"))
+            unpack_products()
+        for k in range(3):
+            (cp if t else act)(V("psc", 128 * k, 128 * k + 128), V("psP", 512 * k, 512 * k + 128))
+
+        def unpack(b):
+            act(V("fh", CW * b, CW * b + 384), V("psE", 512 * b, 512 * b + 384), 0.5)
+
+        def which(src, n, k):
+            for x in range(2):
+                end = n * x + n - 1
+                act(V("junk", 16 * (k + x), 16 * (k + x) + n), V(src, n * x, end + 1), -1.0, F.Sign, V(src, end, end + 1), V("ix", k + x, k + x + 1))
+
+        tt(V("gm"), ind(V("psc"), V("nl")), V("cap"), A.min)
+        if t == 0:
+            tt(V("win1", 290, 314), V("nlf"), V("k2i"), A.add)
+            for x in range(2):
+                act(V("win1", 314 + 14 * x, 326 + 14 * x), V("nlf", 12 * x, 12 * x + 12), bias=-4096.0)
+                act(V("win1", 326 + 14 * x, 327 + 14 * x), p16, bias=384.0 + 16 * x - 4096.0)
+            penalties()
+            weights()
+            table_p()
+            table_b()
+            for x in range(4):
+                act(V("k2c", 13 * x, 13 * x + 12), V("win1", 290 + 12 * (x % 2), 302 + 12 * (x % 2)))
+            for b in range(4):
+                quant(V("eq", 128 * b, 128 * b + 128), V("es", 128 * b, 128 * b + 128), V("et", 3 - b, 515 - b))
+            unpack_products()
+        for b in range(4):
+            unpack(b)
+        scan(V("sc"), V("rs2"), V("gm"), -BIG, A.min, A.max)
+        scan(V("pm1"), V("rs24"), V("sc", 15, 384, 16), -BIG, A.min, A.max)
+        which("pm1", 12, 0)
+        for x in range(2):
+            cp(V("pen", 182 * x + 13, 182 * x + 13 + 155, 14), V("sc", 192 * x + 15, 192 * x + 192, 16))
+        for x in range(2):
+            ts(V("h1", 182 * x, 182 * x + 182), V("we"), V("ix", x, x + 1), A.is_gt)
+        scan(V("s2"), V("h1"), V("pen", 0, 364), 0.0, A.mult, A.add)
+        scan(V("pm2"), V("rs26"), V("s2", 13, 364, 14), -BIG, A.min, A.max)
+        which("pm2", 13, 2)
+        scan(V("kk", 0, 364), V("h1"), V("bt", 0, 364), 0.0, A.mult, A.add)
+        for x in range(2):
+            ts(V("h2", 182 * x, 182 * x + 182), V("we"), V("ix", 2 + x, 3 + x), A.is_gt)
+        scan(V("kk", 364, 728), V("h2"), V("bt", 0, 364), 0.0, A.mult, A.add)
+        tt(V("ka", 52, 104), V("k2c"), V("kk", 12, 728, 14), A.subtract)
+        act(V("ka", 0, 52), V("kk", 13, 728, 14))
+        ts(V("oK"), V("kk", 181, 728, 182), 4096.0, A.add)
+        for b in range(4):
+            act(V("sb", 3 * b + 1, 768, 12), ind(V("fh", CW * b, CW * b + CW), V("oK")), 2.0)
+        scan(V("pmb", 1, 105), V("rsk"), V("ka"), -BIG, A.min, A.max)
+        ts(V("di", 0, 8), V("pmb", 12, 105, 13), 384.0, A.max)
+        tt(V("mn"), V("ka"), V("pmb", 0, 104), A.min)
+        ts(V("dj", 0, 8), V("di", 0, 8), 511, A.bitwise_and)
+        scan(V("sm"), V("rsk"), V("mn"), -BIG, A.min, A.max)
+        cp(V("oA"), V("dj", 0, 8))
+        for b in range(4):
+            act(V("ga", 128 * b, 128 * b + 128), ind(V("fh", CW * b, CW * b + CW), V("oA")))
+        ts(V("di", 8, 16), V("sm", 11, 104, 13), 384.0, A.max)
+        ts(V("dj", 8, 16), V("di", 8, 16), 511, A.bitwise_and)
+        cp(V("oB"), V("dj", 8, 16))
+        for b in range(4):
+            for k in range(2):
+                tt(V("sa", 3 * b + k, 768, 12), ind(V("fh", CW * b, CW * b + CW), V("oB", 4 * k, 4 * k + 4)), V("ga", 128 * b + 64 * k, 128 * b + 64 * k + 64), A.add)
+        scan(V("sy"), V("sa"), V("sb"), -BIG, A.max, A.subtract)
+        cp(V("yt", 0, 256), V("sy", 1, 768, 3))
+        quant(V("yc%d" % t), V("yp%d" % t), V("yt"))
+        src, dst, ca, cb = route(T, topo, rank)
+        sent = post([(dst if k is None else k, (out if k is None else mid) + str(t), mine + str(t), sem + str(t))
+                     for k, sem, mid, out, mine in ((ca, "ac", "rc", "lc", "yc"), (cb, "ap", "rp", "lp", "yp"))])
+        for f in range(2):
+            for x in range(2):
+                ts(V("oo", 26 * f + 13 * x, 26 * f + 13 * x + 13), V("it13"), V("ix", 2 * f + x, 2 * f + x + 1), A.is_equal, -2.0, A.mult)
+        ts(V("pp"), V("kk", 12, 728, 14), -1.0 / Q, A.mult, 0.0, A.max)
+        ts(V("nn"), V("kk", 12, 728, 14), 1.0 / Q, A.mult, 0.0, A.max)
+        if t == 0:
+            ts(V("pd", 3, 4), pt, 26.0, A.mult, p4, A.add)
+            ts(V("pd", 4, 5), p1, -52.0, A.mult, 26.0, A.add)
+            tt(V("uX"), V("uX"), V("uC"), A.add)
+            ts(V("pd", 6, 7), pt, 26.0, A.mult, V("pd", 4, 5), A.add)
+            ts(V("LI"), V("uY"), V("pd", 3, 4), A.add)
+            ts(V("LJ"), V("uX"), V("pd", 6, 7), A.add)
+        tt(V("w", 26, 78), V("pp"), V("oo"), A.add)
+        for f in range(2):
+            tt(V("w", 78 * f, 78 * f + 26), V("nn", 26 * f, 26 * f + 26), V("oo", 26 * f, 26 * f + 26), A.add)
+        if t == 0:
+            fill(V("sg"), -1.0)
+            quant(V("zq"), V("zs"), V("zt"))
+            fill(V("sg", 0, 576, 4), 0.0)
+            fill(V("sg", 2, 576, 4), 1.0)
+            for k in range(R):
+                dma("y", u8(T, "lc%d" % k, 64, 128), u8(T, "zq", 64, 128), V("zq")[1], V("lc%d" % k, 64, 128)[1])
+                dma("y", u8(T, "lp%d" % k, 64, 128), u8(T, "zs", 64, 128), V("zs")[1], V("lp%d" % k, 64, 128)[1])
+        for b in range(4):
+            act(V("y32", 64 * b, 64 * b + 64), V("yt", b, 256, 4), 32.0)
+        half = ((0, 18), (18, 36))
+        for a, b in half:
+            act(V("ei", 16 * a, 16 * b), ind(V("w"), V("LI", a, b)))
+        for b in range(4):
+            act(V("fx", b, 1536, 4), V("fh", CW * b, CW * b + 384), 2.0)
+        for b in range(4):
+            ts(V("so", 4 * b, 4 * b + 4), V("kk", 181, 728, 182), 4.0, A.mult, 16384.0 + b, A.add)
+        for a, b in half:
+            tt(V("pr", 16 * a, 16 * b), ind(V("w"), V("LJ", a, b)), V("ei", 16 * a, 16 * b), A.mult)
+        scan(V("s5"), V("sg"), V("pr"), 0.0, A.mult, A.add)
+        tt(V("sp"), V("s5", 3, 576, 4), V("pw"), A.add)
+        ts(V("pw"), V("sp"), -3.0, A.max, 3.0, A.min)
+        if t < R - 1:
+            penalties()
+            weights()
+            table_p()
+            table_b()
+        else:
+            act(V("win1", 0, 144), V("pw"))
+            act(V("win1", 144, 288), V("pw"), -1.0)
+            act(V("tb1"), ind(V("win1"), L0))
+            for x in range(2):
+                for e in range(12):
+                    act(V("ob", 144 * x + e, 144 * x + 144, 12), V("tb1", 182 * x + e, 182 * x + 168, 14))
+            dma("y", T.oa[:], T.ob[:], V("ob")[1], [])
+            quant(V("vq"), V("vs"), V("vt0"))
+        sender, arr = route(T, topo, (rank - 1) % N), []
+        for sem, k in (("ac%d" % t, sender[2]), ("ap%d" % t, sender[3])):
+            arr.append((sem, len(topo.engines(sender[0] if k is None else k, core))))
+        for b in range(4):
+            mm(V("psE", 512 * b, 512 * b + 128), V("wq", 128 * b, 128 * b + 128), V("wp", 128 * b, 128 * b + 128), V("lc%d" % t), V("lp%d" % t), (sent, arr))
+        for b in range(4):
+            tt(V("vf", 64 * b, 64 * b + 64), V("psE", 512 * b, 512 * b + 64), V("y32", 64 * b, 64 * b + 64), A.add)
+            ts(V("vt", 64 * b, 64 * b + 64), V("vf", 64 * b, 64 * b + 64), 0.03125, A.mult)
+        run("v", lambda e: e.tensor_copy(T.fx[:, 0:1664].indirect(T.so[:, 0:16]), T.vt[:]), [V("vt"), V("so")], [V("fx")], 1000.0)
+
+    score_products(V("vq"), V("vs"))
+    dma("y", T.oc[:], u8(T, "xq", 0, 384), V("xq")[1], [])
+    for k in range(4):
+        dma("y", T.osc[4 * k:4 * k + 4, :], T.xs[32 * k:32 * k + 4, :], V("xs")[1], [])
+    for k in range(3):
+        cp(V("ysb", 128 * k, 128 * k + 128), V("psP", 512 * k, 512 * k + 128))
+    dma("s", T.y[:], T.ysb[:], V("ysb")[1], [])
+    issue()
+    for sem in count:
+        need("g", sem, count[sem], {})

@@ -2,10 +2,11 @@ from concourse.mybir import dt, AluOpType, ActivationFunctionType
 
 N, C, R = 8, 384, 3
 BIG = 2.0 ** 90
-PEN, NONE = 2.0 ** 80, 2.0 ** 79
-Q = 8192.0
-CW = 416
-WAKE, NEAR, FAR = 120.0, 3000.0, 6200.0
+NONE = 2.0 ** 79
+Q = 16384.0
+MU = 1.0 / 64
+SHIFT = 192.0
+WAKE, NEAR, FAR = 110.0, 2600.0, 5600.0
 SCRATCH, CODES = {}, set()
 
 
@@ -18,18 +19,18 @@ def declare(dtype, spec):
             CODES.add(name)
 
 
-declare("bfloat16", "fx:1664 fh:1664 ut:512 vt0:512 yt:512 zt:512 et:520 ones:128 ga:512 sa:768 sb:768 sy:768 y32:256 vt:256 "
-        "h1:364 h2:364 pw:144 w:104 pp:52 nn:52 oo:52 ei:576 pr:576 s5:576 sp:144 iC:384 cap:384 we:182 rs2:384 sg:576")
-declare("float8_e4m3fn_x4", "uq:128 urq:128 vq:128 eq:512 zq:128 wq:512 xq:384 " + " ".join("yc%d:128 lc%d:128 rc%d:64" % (t, t, t) for t in range(R)))
-declare("uint8", "us:128 urs:128 vs:128 es:512 zs:128 wp:512 xs:384 " + " ".join("yp%d:128 lp%d:128 rp%d:64" % (t, t, t) for t in range(R)))
-declare("float32", "psP:1536 psE:2048 vf:256 psc:384 gm:384 sc:384 pm1:24 ix:4 junk:64 s2:364 pm2:26 kk:728 ka:104 pmb:105 mn:104 sm:104 "
-        "bt:368 pen:368 win1:344 win2:344 tb1:368 tp0:368 ob:288 ysb:384 rt:384 iK:384 nlf:24 pf:4 pd:8 it13:13 k2i:24 k2c:52 "
-        "rsx:160 lm:46 lA:46 lB:46 lC:46 lD:46 lE:46 lF:46 lG:46 lH:46 lI:46 uA:36 uX:36 uY:36 uZ:36 uB:36 uC:36")
-declare("int32", "di:16 dj:16 ndi:24 ari:288 pI:4 pA:4 ui:8 li:46")
-declare("uint16", "oL:20 so:16 nd16:24 nl:24 ul:8 L:156")
-PART = {"oA": ("oL", 0, 8), "oB": ("oL", 8, 8), "oK": ("oL", 16, 4), "rs24": ("rsx", 0, 24), "rs26": ("rsx", 24, 26), "rsk": ("rsx", 52, 104),
-        "LI": ("L", 48, 36), "LJ": ("L", 84, 36), "L4": ("L", 120, 36)}
-DMAS = 26
+declare("bfloat16", "fx:1664 ut:512 vt0:512 yt:512 zt:512 et:520 ones:128 ga:512 sa:768 sb:768 sy:768 y32:256 v32:256 vt:256 "
+        "hm:676 we:170 tb:352 df:338 kr:676 win:304 bs:144 sp:144 pr:720 s5:720 sg:720 sta:128 stb:192 w:192 pp:52 nn:52 oo:52 "
+        "iC:400 cap:400 rs2:400")
+declare("float8_e4m3fn_x4", "uq:128 urq:128 vq:128 eq:512 zq:128 wq:512 xq:384 lc:448 " + " ".join("yc%d:128 rc%d:64" % (t, t) for t in range(R)))
+declare("uint8", "us:128 urs:128 vs:128 es:512 zs:128 wp:512 xs:384 lp:448 " + " ".join("yp%d:128 rp%d:64" % (t, t) for t in range(R)))
+declare("float32", "psP:1536 psE:2048 psc:416 gm:400 sc:400 pm1:26 pm2:26 pen:26 s2:26 rs25:26 ix:4 junk:64 ka:104 ps:260 rsk:52 "
+        "k2i:26 k2c:26 nlf:28 nq:28 dk:26 ob:300 ysb:384 rt:384 iK:384 pf:4 pd:4 "
+        "lm:22 lA:22 lB:22 lC:22 lD:22 lE:22 lF:22 lG:22 lH:22 uA:9 uB:9 uC:9 uD:9 uE:9 "
+        "mA:12 mB:12 mC:12 mD:24 mE:12 mF:12")
+declare("int32", "di:20 dj:20 ndi:24 ari:288 pI:4 pA:4 ui:8 li:22 mi:12 mj:24")
+declare("uint16", "gl:80 so:16 nd16:24 nl:26 ul:8 LT:22 LP:10 La:8 Lb:12")
+DMAS = 34
 SEMAPHORES = ["qv", "qs", "qt", "qg", "sent"] + ["d%d" % i for i in range(DMAS)] + ["ac%d" % t for t in range(R)] + ["ap%d" % t for t in range(R)]
 
 
@@ -47,9 +48,9 @@ def u8(T, name, a, b):
     return v.bitcast(dt.uint8) if name in CODES else v
 
 
-def send(g, T, topo, core, to, out, src, sem):
+def send(g, T, topo, core, to, out, at, src, sem):
     rid, pid = topo.addr(to, core)
-    g.remote_dma(u8(T, out, 0, 64), u8(T, src, 0, 64), T.sem[sem], T.sem.sent, pid, rid, topo.mask(core, to))
+    g.remote_dma(u8(T, out, at, at + 64), u8(T, src, 0, 64), T.sem[sem], T.sem.sent, pid, rid, topo.mask(core, to))
     return len(topo.engines(core, to))
 
 
@@ -58,10 +59,10 @@ def relay_program(g, core, T, topo):
     for t in range(R):
         for r in range(N):
             src, dst, ca, cb = route(T, topo, r)
-            for k, sem, mid, out in ((ca, "ac%d" % t, "rc%d" % t, "lc%d" % t), (cb, "ap%d" % t, "rp%d" % t, "lp%d" % t)):
+            for k, sem, mid, out in ((ca, "ac%d" % t, "rc%d" % t, "lc"), (cb, "ap%d" % t, "rp%d" % t, "lp")):
                 if k == core:
                     g.wait_ge(T.sem[sem], len(topo.engines(src, core)))
-                    total += send(g, T, topo, core, dst, out, mid, sem)
+                    total += send(g, T, topo, core, dst, out, 64 + 128 * t, mid, sem)
     if total:
         g.wait_ge(T.sem.sent, total)
 
@@ -92,7 +93,7 @@ def rank_program(g, core, T, topo):
         for kind, regions in (("r", reads), ("w", writes)):
             for x in regions:
                 for o, y, d in last.get(x[0], []):
-                    if (kind == "w" or o == "w") and overlap(x, y):
+                    if (kind == "w" or o == "w" or x[0] in ("psP", "psE") and ops[d][0] != q) and overlap(x, y):
                         deps.setdefault(d, 0.0)
         for x in writes:
             last[x[0]] = [e for e in last.get(x[0], []) if not (e[1][1] >= x[1] and e[1][2] <= x[2] and x[3] == 1)]
@@ -103,21 +104,21 @@ def rank_program(g, core, T, topo):
         return k
 
     def run(q, call, reads, writes, cost, arr=None):
-        reads = [x for o in reads for x in o[1]]
-        writes = [x for o in writes for x in o[1]]
-        both = [x for x in reads if x[0] in ("psP", "psE")]
-        add(q, lambda e: call(e).then_inc(T.sem["q" + q], 1), [x for x in reads if x not in both], writes + both, cost,
-            after=[arr[0]] if arr else (), arrivals=arr[1] if arr else (), lag=(NEAR if direct else FAR) if arr else 0.0)
+        bank = lambda x: (x[0], x[1] // 512 * 512, x[1] // 512 * 512 + 512, 1) if x[0] in ("psP", "psE") else x
+        reads = [bank(x) for o in reads for x in o[1]]
+        writes = [bank(x) for o in writes for x in o[1]]
+        add(q, lambda e: call(e).then_inc(T.sem["q" + q], 1), reads, writes, cost,
+            after=[arr[0]] if arr else (), arrivals=arr[1] if arr else (), lag=arr[2] if arr else 0.0)
 
-    def dma(q, out, in_, reads, writes):
+    def dma(q, out, in_, reads, writes, cost=2400.0):
         sem = free.pop(0)
-        add(q, lambda e: e.dma_start(out, in_).then_inc(T.sem[sem], 16), reads, writes, 2700.0, sem, 16)
+        add(q, lambda e: e.dma_start(out, in_).then_inc(T.sem[sem], 16), reads, writes, cost, sem, 16)
 
     def post(writes):
         def call(e):
-            for to, out, mine, sem in writes:
-                count["sent"] = count.get("sent", 0) + send(e, T, topo, core, to, out, mine, sem)
-        return add("g", call, [(w[2], 0, 128, 1) for w in writes], [], 1400.0, "sent", 0)
+            for to, out, at, mine, sem in writes:
+                count["sent"] = count.get("sent", 0) + send(e, T, topo, core, to, out, at, mine, sem)
+        return add("g", call, [(w[3], 0, 128, 1) for w in writes], [], 1400.0, "sent", 0)
 
     def issue():
         n = len(ops)
@@ -164,9 +165,7 @@ def rank_program(g, core, T, topo):
                 known[q][s] = max(known[q].get(s, 0), clock[s])
 
     def V(name, a=0, b=None, step=1):
-        name, o, n = PART.get(name, (name, 0, None))
-        b = (SCRATCH[name][1][1] if n is None else n) if b is None else b
-        a, b = a + o, b + o
+        b = SCRATCH[name][1][1] if b is None else b
         return (T[name][:, a:b:step] if step > 1 else T[name][:, a:b], [(name, a, b, step)])
 
     def ind(win, off):
@@ -183,11 +182,11 @@ def rank_program(g, core, T, topo):
         return (b - a + step - 1) // step
 
     def fast(n, *v):
-        return max(64, n * (0.5 if all(SCRATCH[x[1][0][0]][2] in ("bfloat16", "uint16") for x in v) else 1))
+        return max(66, 1.04 * n * (0.5 if all(SCRATCH[x[1][0][0]][2] in ("bfloat16", "uint16") for x in v) else 1))
 
     def tt(out, a, b, op):
         n = size(out)
-        cost = 50 + 1.6 * n if len(a) > 2 else max(64, n if a[1][0][0] in ("psP", "psE") else 2 * n)
+        cost = 50 + 1.62 * n if len(a) > 2 else max(66, 1.04 * (n if a[1][0][0] in ("psP", "psE") else 2 * n))
         run("v", lambda e: e.tensor_tensor(out[0], a[0], b[0], op), [a, b], [out], cost)
 
     def ts(out, a, s1, op0, s2=None, op1=None):
@@ -200,16 +199,16 @@ def rank_program(g, core, T, topo):
         run("v", lambda e: e.tensor_copy(out[0], a[0]), [a], [out], fast(size(out), a, out))
 
     def scan(out, d0, d1, initial, op0, op1):
-        run("v", lambda e: e.tensor_tensor_scan(out[0], d0[0], d1[0], initial, op0, op1), [d0, d1], [out], fast(size(out), d0, d1, out))
+        run("v", lambda e: e.tensor_tensor_scan(out[0], d0[0], d1[0], val(initial), op0, op1), [d0, d1] + reg(initial), [out], fast(size(out), d0, d1, out))
 
     def fill(out, c):
-        run("v", lambda e: e.memset(out[0], c), [], [out], max(64, size(out)))
+        run("v", lambda e: e.memset(out[0], c), [], [out], fast(size(out), out))
 
     def quant(q, s, t):
-        run("v", lambda e: e.quantize_mx(q[0], s[0], t[0]), [t], [q, s], 15 + 0.26 * size(t))
+        run("v", lambda e: e.quantize_mx(q[0], s[0], t[0]), [t], [q, s], 15 + 0.275 * size(t))
 
-    def mm(out, w, ws, x, xs, arr=None):
-        run("t", lambda e: e.matmul_mx(out[0], w[0], ws[0], x[0], xs[0], True, True), [w, ws, x, xs], [out], 1.7 * size(x) + 18, arr)
+    def mm(out, w, ws, x, xs):
+        run("t", lambda e: e.matmul_mx(out[0], w[0], ws[0], x[0], xs[0], True, True), [w, ws, x, xs], [out], 1.3 * size(x) + 20)
 
     def act(out, a, scale=1.0, func=None, bias=None, accum=None):
         kw = {}
@@ -221,86 +220,64 @@ def rank_program(g, core, T, topo):
         if accum is not None:
             kw["accum_out"] = accum[0]
         run("s", lambda e: e.activation(out[0], a[0], func or F.Copy, **kw), [a] + reg(bias), [out] + reg(accum),
-            70 + 1.6 * size(out) if len(a) > 2 else max(64, size(out)) + (20 if accum is not None else 0))
+            65 + 1.62 * size(out) if len(a) > 2 else max(66, 1.04 * size(out)) + (20 if accum is not None else 0))
 
     def iota(out, pattern, base=0, cm=0):
-        cost = 150 + 2 * size(out)
+        cost = 130 + 2.1 * size(out)
         if SCRATCH[out[1][0][0]][2] == "int32":
             run("g", lambda e: e.iota(out[0], pattern, base, cm), [], [out], cost)
         else:
             run("g", lambda e: e.iota(out[0], pattern, base, cm, allow_small_or_imprecise_dtypes=True), [], [out], cost)
 
-    def select(out, pattern, fill_, base):
-        run("g", lambda e: e.affine_select(out[0], out[0], pattern, A.not_equal, fill_, base, 0), [out], [out], 200 + 2 * size(out))
+    dma("y", T.ndi[:], T.nd[:], [], V("ndi")[1], 2100.0)
+    dma("s", T.ut[:], T.u[:], [], V("ut")[1], 2800.0)
+    for k, q in enumerate("ysy"):
+        dma(q, T.fx[:, 512 * k:512 * k + 512], T.x[:, 512 * k:512 * k + 512], [], V("fx", 512 * k, 512 * k + 512)[1], 2900.0 + 300 * k)
+    dma("s", T.ari[:], T.ar[:], [], V("ari")[1], 4000.0)
 
-    dma("y", T.ndi[:], T.nd[:], [], V("ndi")[1])
-    dma("s", T.ut[:], T.u[:], [], V("ut")[1])
-    dma("y", T.fx[:, 0:768], T.x[:, 0:768], [], V("fx", 0, 768)[1])
-    dma("s", T.fx[:, 768:1536], T.x[:, 768:1536], [], V("fx", 768, 1536)[1])
-    dma("y", T.ari[:], T.ar[:], [], V("ari")[1])
-    dma("y", T.wq[:, 0:512].bitcast(dt.uint8), T.wc[:], [], V("wq")[1])
-    dma("y", T.wp[:], T.ws[:], [], V("wp")[1])
-    dma("y", T.vt0[:], T.v[:], [], V("vt0")[1])
-
-    lm = lambda n, a=0, b=46: V(n, a, b)
     iota(V("pI"), [[0, 4]], 0, 1)
-    iota(lm("lm"), [[0, 2], [16, 23]])
-    iota(V("uA"), [[0, 2], [1, 6], [4, 3]], 1)
-    iota(V("uZ"), [[144, 2], [0, 6], [48, 3]])
     iota(V("iK"), [[1, 384]])
-    iota(V("iC"), [[0, 24], [1, 16]])
     iota(V("ui"), [[16, 8]])
-    iota(V("ones"), [[0, 128]], 1)
-    iota(V("et"), [[0, 520]])
-    run("g", lambda e: e.affine_select(T.et[:, 3:515:4], T.ones[:], [[-1, 128]], A.is_equal, 0.0, 0, 1), [V("ones")], [V("et")], 460.0)
-    iota(V("k2i"), [[0, 2], [-512, 12]], -512)
-    for n in ("win1", "win2"):
-        iota(V(n, 288, 344), [[0, 56]])
-    act(V("rsx"), V("iC", 0, 160), 0.0, bias=BIG)
-    for k, c in ((1, PEN), (39, NONE), (53, NONE)):
-        select(V("win2", 288, 344), [[1, 56]], c, -k)
-    select(V("rs24"), [[0, 2], [1, 12]], -BIG, 0)
-    select(V("rs26"), [[0, 2], [1, 13]], -BIG, 0)
-    iota(V("we"), [[0, 13], [1, 14]])
-    iota(V("k2c"), [[0, 52]], -8192)
-    select(V("rsk"), [[0, 8], [1, 13]], -BIG, -12)
-    for b in range(4):
-        iota(V("fh", CW * b + 384, CW * b + CW), [[0, 32]])
+    iota(V("lm"), [[16, 22]])
+    iota(V("uA"), [[0, 3], [8, 3]])
+    iota(V("uB"), [[2, 3], [0, 3]], 1)
+    iota(V("iC"), [[0, 25], [1, 16]])
+    fill(V("ones"), 1.0)
+    fill(V("et"), 0.0)
+    run("g", lambda e: e.affine_select(T.et[:, 3:515:4], T.ones[:], [[-1, 128]], A.is_equal, 0.0, 0, 1), [V("ones")], [V("et")], 440.0)
+    iota(V("k2i"), [[0, 2], [-512, 13]], int(512 * 13 - Q))
+    iota(V("k2i", 0, 26, 13), [[0, 2]])
+    iota(V("we", 0, 169), [[0, 13], [1, 13]])
+    iota(V("psc", 384, 416), [[0, 32]])
+    iota(V("fx", 1536, 1664), [[0, 128]])
     iota(V("yt", 256, 512), [[0, 256]])
-    iota(V("uX"), [[13, 2], [0, 18]])
-    iota(V("uY"), [[13, 2], [0, 6], [4, 3]])
-    iota(V("it13"), [[1, 13]])
     iota(V("sb", 0, 768, 3), [[0, 256]])
+    iota(V("zt"), [[0, 512]])
+    iota(V("w"), [[0, 192]])
+    iota(V("win", 288, 304), [[0, 16]])
+    act(V("win", 288, 289), V("win", 289, 290), bias=MU)
+    iota(V("sg"), [[0, 720]], 1)
+    iota(V("sg", 0, 720, 5), [[0, 144]])
+    iota(V("sg", 3, 720, 5), [[0, 144]], -1)
     act(V("sa", 2, 768, 3), V("iC", 0, 256), 0.0, bias=-BIG)
     act(V("sb", 2, 768, 3), V("iC", 0, 256), 0.0, bias=BIG)
-    iota(V("zt"), [[0, 512]])
+    act(V("rs25"), V("iC", 0, 26), 0.0, bias=BIG)
+    act(V("rs25", 12, 13), V("iC", 0, 1), 0.0, bias=-NONE)
+    act(V("rsk"), V("iC", 0, 52), 0.0, bias=BIG)
+    act(V("rsk", 0, 52, 13), V("iC", 0, 4), 0.0, bias=-BIG)
+    for n in ("pm1", "pm2"):
+        act(V(n, 0, 1), V("iC", 0, 1), 0.0, bias=-NONE)
+    act(V("k2i"), V("k2i"), 1.0 / Q)
 
     ts(V("pA", 0, 1), V("pI", 0, 1), 15, A.bitwise_and)
-    ts(V("pA", 1, 2), V("pI", 1, 2), 2, A.logical_shift_right, 3, A.bitwise_and)
-    ts(V("pA", 2, 3), V("pI", 2, 3), 3, A.bitwise_and)
-    ts(V("pA", 3, 4), V("pI", 3, 4), 1, A.bitwise_and)
-    cp(V("pf"), V("pA"))
-    p16, p4, pt, p1 = (V("pf", k, k + 1) for k in range(4))
-    act(V("pd", 2, 3), p16, -1.0, bias=182.0)
-    act(V("pd", 5, 6), p4, 12.0)
-    act(V("uB"), V("uA"), bias=p4)
-    ts(lm("lB"), lm("lm"), V("pd", 2, 3), A.is_ge)
-    ts(lm("lC"), lm("lB"), -182.0, A.mult, p16, A.add)
-    ts(V("uC"), V("uB"), 12.0, A.is_ge, -12.0, A.mult)
-    tt(lm("lD"), lm("lC"), lm("lm"), A.add)
-    tt(V("uC"), V("uC"), V("uB"), A.add)
-    ts(lm("li"), lm("lD"), 1.0 / 14, A.mult, -6.5 / 14, A.add)
-    act(V("pmb", 0, 1), p16, 0.0, bias=-BIG)
-    cp(lm("lE"), lm("li"))
-    tt(V("uZ"), V("uZ"), V("uC"), A.add)
-    ts(lm("lC"), lm("lE"), -14.0, A.mult)
-    ts(V("L4"), V("uZ"), V("pd", 5, 6), A.add)
-    tt(lm("lF"), lm("lC"), lm("lD"), A.add)
-    ts(lm("lF", 23, 46), lm("lF", 23, 46), 1.0, A.add)
-    tt(lm("lC"), lm("lF"), lm("lE"), A.subtract)
-    act(lm("lI"), lm("lB"), 72.0)
-    ts(lm("lD"), lm("lC"), 0.0, A.is_lt, 12.0, A.mult)
-    tt(lm("lC"), lm("lC"), lm("lD"), A.add)
+    ts(V("pA", 1, 2), V("pI", 1, 2), 1, A.logical_shift_right, 7, A.bitwise_and)
+    ts(V("pA", 2, 3), V("pI", 2, 3), 1, A.bitwise_and)
+    cp(V("pf", 0, 3), V("pA", 0, 3))
+    p16, p8, p1 = (V("pf", k, k + 1) for k in range(3))
+    for k, c in ((0, 384.0), (13, 400.0)):
+        act(V("nlf", k, k + 1), p16, bias=c)
+    act(V("nlf", 26, 28), V("pf", 0, 2), 0.0)
+    act(V("pd", 0, 1), p1, 144.0)
 
     def score_products(w, ws):
         for k in range(3):
@@ -315,204 +292,209 @@ def rank_program(g, core, T, topo):
     cp(V("nd16"), V("ndi"))
     act(V("rt"), ind(V("iK"), V("nd16")))
     for x in range(2):
-        dma("y", T.nlf[:, 12 * x:12 * x + 12], T.rt[0:128:16, 192 * x:192 * x + 192], V("rt")[1], V("nlf", 12 * x, 12 * x + 12)[1])
+        dma("ys"[x], T.nlf[:, 13 * x + 1:13 * x + 13], T.rt[0:128:16, 192 * x:192 * x + 192], V("rt")[1] + [("nlf", 0, 28, 13)],
+            [("nlf", 13 * x + 1, 13 * x + 13, 1)], 2100.0)
+    dma("y", T.wq[:, 0:512].bitcast(dt.uint8), T.wc[:], V("nlf")[1], V("wq")[1], 4000.0)
+    dma("y", T.wp[:], T.ws[:], V("nlf")[1], V("wp")[1])
+    dma("y", T.vt0[:], T.v[:], V("nlf")[1], V("vt0")[1])
     act(V("cap"), V("iC"), -1.0, F.Square, p16)
-    act(V("cap"), V("cap"), -2.0 * BIG, bias=BIG)
-    act(V("rs2"), V("iC"), 0.0, bias=BIG)
+    ts(V("cap"), V("cap"), -2.0 * BIG, A.mult, BIG, A.add)
+    fill(V("cap", 192, 208), -BIG)
+    fill(V("rs2"), BIG)
     cp(V("ul"), V("ui"))
-    fill(V("rs2", 0, 384, 16), -BIG)
+    fill(V("rs2", 0, 400, 16), -BIG)
     quant(V("uq"), V("us"), V("ut"))
     run("v", lambda e: e.tensor_copy(T.urq[:, 0:128].bitcast(dt.uint32), T.uq[:, 0:128].bitcast(dt.uint32).indirect(T.ul[:, 0:8])),
-        [V("uq"), V("ul")], [V("urq")], 250.0)
+        [V("uq"), V("ul")], [V("urq")], 260.0)
     act(V("urs"), ind(V("us"), V("ul")))
-    score_products(V("urq"), V("urs"))
-    act(V("ei"), ind(V("ari"), V("L4")))
-    act(V("pw"), V("ei", 0, 576, 4))
-    cp(V("nl"), V("nlf"))
-    act(lm("lG"), lm("lC"), 12.0, bias=-12.0)
-    act(lm("lD"), lm("lC"), -12.0, bias=276.0)
-    ts(lm("lH"), lm("lC"), 7.0, A.is_ge, 1000.0, A.mult)
-    tt(lm("lG"), lm("lG"), lm("lE"), A.add)
-    tt(lm("lD"), lm("lD"), lm("lF"), A.add)
-    tt(lm("lG"), lm("lG"), lm("lH"), A.add)
-    ts(lm("lH"), lm("lC"), 0.0, A.is_equal, 289.0, A.mult)
-    tt(lm("lG"), lm("lG"), lm("lD"), A.min)
-    tt(lm("lG"), lm("lG"), lm("lI"), A.add)
-    tt(lm("lG"), lm("lG"), lm("lH"), A.max)
-    e0, e1 = lm("lF", 0, 23), lm("lF", 23, 46)
-    act(lm("lA"), lm("lB"), 14.0, bias=314.0)
-    act(lm("lC", 0, 23), lm("lB", 0, 23), 12.0, bias=290.0)
-    ts(lm("lH"), lm("lF"), 12.0, A.is_ge, 288.0, A.mult)
-    ts(lm("lI"), lm("lE"), 12.0, A.is_equal)
-    tt(lm("lG"), lm("lG"), lm("lH"), A.max)
-    tt(lm("lA"), lm("lA"), lm("lF"), A.add)
-    tt(lm("lC", 0, 23), lm("lC", 0, 23), lm("lE", 0, 23), A.add)
-    ts(lm("lD", 0, 23), e0, 13.0, A.is_equal)
-    ts(lm("lD", 23, 46), e1, 13.0, A.is_lt)
-    tt(lm("lA"), lm("lA"), lm("lI"), A.mult)
-    tt(lm("lC", 0, 23), lm("lC", 0, 23), lm("lD", 0, 23), A.mult)
-    tt(lm("lA", 23, 46), lm("lA", 23, 46), lm("lD", 23, 46), A.mult)
-    tt(lm("lG", 0, 23), lm("lG", 0, 23), lm("lC", 0, 23), A.max)
-    tt(lm("lG"), lm("lG"), lm("lA"), A.max)
-    cp(V("L", 0, 23), lm("lG", 0, 23))
-    cp(V("L", 24, 47), lm("lG", 23, 46))
-    L0, L1 = V("L", 0, 23), V("L", 24, 47)
+    for b in range(4):
+        quant(V("eq", 128 * b, 128 * b + 128), V("es", 128 * b, 128 * b + 128), V("et", 3 - b, 515 - b))
+    cp(V("nl", 0, 25), V("nlf", 1, 26))
+    act(V("nq"), V("nlf"), 1.0 / Q)
+    tt(V("k2c"), V("nq", 0, 26), V("k2i"), A.add)
+    tt(V("dk"), V("nq", 0, 26), V("nq", 1, 27), A.subtract)
+    act(V("dk", 12, 13), V("nq", 12, 13))
 
-    def penalties():
-        act(V("win2", 0, 144), V("pw"), PEN, F.Abs)
-        act(V("win2", 144, 288), V("pw"), PEN, F.Abs)
-        act(V("tp0"), ind(V("win2"), L0))
+    act(V("uA"), V("uA"), bias=p8)
+    ts(V("uC"), V("uA"), 12.0, A.is_ge)
+    act(V("uD"), V("uC"), -12.0)
+    tt(V("uB"), V("uB"), V("uC"), A.add)
+    tt(V("uA"), V("uA"), V("uD"), A.add)
+    tt(V("uB"), V("uB"), V("uA"), A.add)
+    ts(V("uE"), V("uA"), 12.0, A.mult, V("pd", 0, 1), A.add)
+    ts(V("uC"), V("uB"), 12.0, A.is_ge, -12.0, A.mult)
+    tt(V("uE"), V("uE"), V("uB"), A.add)
+    tt(V("uE"), V("uE"), V("uC"), A.add)
+    cp(V("LP", 0, 9), V("uE"))
+    act(V("win", 0, 144), ind(V("ari"), V("LP", 0, 9)))
+    act(V("win", 144, 288), V("win", 0, 144), -1.0)
+    act(V("bs"), V("win", 0, 144), bias=-SHIFT)
 
-    def weights():
-        act(V("win1", 0, 144), V("pw"), Q)
-        act(V("win1", 144, 288), V("pw"), -Q)
-        act(V("tb1"), ind(V("win1"), L1))
+    act(V("lm"), V("lm"), bias=p16)
+    ts(V("li"), V("lm"), 1.0 / 13, A.mult, -6.0 / 13, A.add)
+    ts(V("lB"), V("lm"), 169.0, A.is_ge)
+    cp(V("lA"), V("li"))
+    act(V("lC"), V("lB"), -13.0)
+    act(V("lD"), V("lA"), -13.0)
+    tt(V("lA"), V("lA"), V("lC"), A.add)
+    tt(V("lD"), V("lD"), V("lm"), A.add)
+    tt(V("lC"), V("lA"), V("lD"), A.subtract)
+    tt(V("lH"), V("lA"), V("lD"), A.mult)
+    ts(V("lE"), V("lC"), 0.0, A.is_lt, 12.0, A.mult)
+    act(V("lD"), V("lD"), 2.0, bias=-26.0)
+    act(V("lA"), V("lA"), 2.0, bias=406.0)
+    tt(V("lC"), V("lC"), V("lE"), A.add)
+    ts(V("lH"), V("lH"), 0.0, A.is_equal, 289.0, A.mult)
+    act(V("lE"), V("lC"), 24.0)
+    ts(V("lF"), V("lC"), 7.0, A.is_ge, 1000.0, A.mult)
+    ts(V("lG"), V("lC"), 0.0, A.is_equal, 288.0, A.mult)
+    tt(V("lD"), V("lD"), V("lE"), A.add)
+    tt(V("lA"), V("lA"), V("lE"), A.subtract)
+    tt(V("lD"), V("lD"), V("lF"), A.add)
+    tt(V("lG"), V("lG"), V("lH"), A.max)
+    tt(V("lD"), V("lD"), V("lA"), A.min)
+    tt(V("lD"), V("lD"), V("lB"), A.add)
+    tt(V("lD"), V("lD"), V("lG"), A.max)
+    ts(V("LT"), V("lD"), 289.0, A.min)
 
-    def table_p():
-        tt(V("pen"), ind(V("win2"), L1), V("tp0"), A.subtract)
+    def table():
+        act(V("tb"), ind(V("win"), V("LT")))
+        for a, b in ((0, 84), (84, 169), (169, 253), (253, 338)):
+            tt(V("df", a, b), V("tb", a, b), V("tb", a + 1, b + 1), A.subtract)
 
-    def table_b():
-        tt(V("bt"), ind(V("win1"), L0), V("tb1"), A.subtract)
+    table()
+
+    def stream_lists():
+        m = V("lm", 0, 12)
+        ts(V("mi"), m, 0.2, A.mult, -0.4, A.add)
+        cp(V("mA"), V("mi"))
+        ts(V("mj", 0, 12), V("mi"), 1, A.bitwise_and)
+        ts(V("mj", 12, 24), V("mi"), 1, A.logical_shift_right)
+        act(V("mA"), V("mA"), -5.0)
+        cp(V("mD"), V("mj"))
+        tt(V("mA"), V("mA"), m, A.add)
+        ts(V("mB"), V("mD", 12, 24), 12.0, A.is_ge, -12.0, A.mult)
+        act(V("mC"), V("mD", 0, 12), 13.0, bias=105.0)
+        act(V("mE"), V("mA"), -26.0)
+        act(V("mF"), V("mA"), 1.0, F.Abs, -1.5)
+        tt(V("mB"), V("mB"), V("mD", 12, 24), A.add)
+        tt(V("mC"), V("mC"), V("mE"), A.add)
+        ts(V("mF"), V("mF"), 1.0, A.is_lt, -104.0, A.mult)
+        tt(V("mC"), V("mC"), V("mB"), A.add)
+        cp(V("Lb"), V("mC"))
+        tt(V("mF"), V("mF"), V("mC"), A.add)
+        ts(V("La"), V("mF", 0, 8), 52.0, A.add)
 
     for t in range(R):
-        if t:
-            score_products(V("urq"), V("urs"))
-            unpack_products()
+        score_products(V("urq"), V("urs"))
+        unpack_products()
         for k in range(3):
-            (cp if t else act)(V("psc", 128 * k, 128 * k + 128), V("psP", 512 * k, 512 * k + 128))
-
-        def unpack(b):
-            act(V("fh", CW * b, CW * b + 384), V("psE", 512 * b, 512 * b + 384), 0.5)
-
-        def which(src, n, k):
-            for x in range(2):
-                end = n * x + n - 1
-                act(V("junk", 16 * (k + x), 16 * (k + x) + n), V(src, n * x, end + 1), -1.0, F.Sign, V(src, end, end + 1), V("ix", k + x, k + x + 1))
-
-        tt(V("gm"), ind(V("psc"), V("nl")), V("cap"), A.min)
-        if t == 0:
-            tt(V("win1", 290, 314), V("nlf"), V("k2i"), A.add)
-            for x in range(2):
-                act(V("win1", 314 + 14 * x, 326 + 14 * x), V("nlf", 12 * x, 12 * x + 12), bias=-4096.0)
-                act(V("win1", 326 + 14 * x, 327 + 14 * x), p16, bias=384.0 + 16 * x - 4096.0)
-            penalties()
-            weights()
-            table_p()
-            table_b()
-            for x in range(4):
-                act(V("k2c", 13 * x, 13 * x + 12), V("win1", 290 + 12 * (x % 2), 302 + 12 * (x % 2)))
-            for b in range(4):
-                quant(V("eq", 128 * b, 128 * b + 128), V("es", 128 * b, 128 * b + 128), V("et", 3 - b, 515 - b))
-            unpack_products()
+            cp(V("psc", 128 * k, 128 * k + 128), V("psP", 512 * k, 512 * k + 128))
         for b in range(4):
-            unpack(b)
+            for h in range(2):
+                act(V("fx", b + 768 * h, 768 * h + 768, 4), V("psE", 512 * b + 192 * h, 512 * b + 192 * h + 192))
+        tt(V("gm"), ind(V("psc"), V("nl", 0, 25)), V("cap"), A.min)
         scan(V("sc"), V("rs2"), V("gm"), -BIG, A.min, A.max)
-        scan(V("pm1"), V("rs24"), V("sc", 15, 384, 16), -BIG, A.min, A.max)
-        which("pm1", 12, 0)
-        for x in range(2):
-            cp(V("pen", 182 * x + 13, 182 * x + 13 + 155, 14), V("sc", 192 * x + 15, 192 * x + 192, 16))
-        for x in range(2):
-            ts(V("h1", 182 * x, 182 * x + 182), V("we"), V("ix", x, x + 1), A.is_gt)
-        scan(V("s2"), V("h1"), V("pen", 0, 364), 0.0, A.mult, A.add)
-        scan(V("pm2"), V("rs26"), V("s2", 13, 364, 14), -BIG, A.min, A.max)
-        which("pm2", 13, 2)
-        scan(V("kk", 0, 364), V("h1"), V("bt", 0, 364), 0.0, A.mult, A.add)
-        for x in range(2):
-            ts(V("h2", 182 * x, 182 * x + 182), V("we"), V("ix", 2 + x, 3 + x), A.is_gt)
-        scan(V("kk", 364, 728), V("h2"), V("bt", 0, 364), 0.0, A.mult, A.add)
-        tt(V("ka", 52, 104), V("k2c"), V("kk", 12, 728, 14), A.subtract)
-        act(V("ka", 0, 52), V("kk", 13, 728, 14))
-        ts(V("oK"), V("kk", 181, 728, 182), 4096.0, A.add)
-        for b in range(4):
-            act(V("sb", 3 * b + 1, 768, 12), ind(V("fh", CW * b, CW * b + CW), V("oK")), 2.0)
-        scan(V("pmb", 1, 105), V("rsk"), V("ka"), -BIG, A.min, A.max)
-        ts(V("di", 0, 8), V("pmb", 12, 105, 13), 384.0, A.max)
-        tt(V("mn"), V("ka"), V("pmb", 0, 104), A.min)
-        ts(V("dj", 0, 8), V("di", 0, 8), 511, A.bitwise_and)
-        scan(V("sm"), V("rsk"), V("mn"), -BIG, A.min, A.max)
-        cp(V("oA"), V("dj", 0, 8))
-        for b in range(4):
-            act(V("ga", 128 * b, 128 * b + 128), ind(V("fh", CW * b, CW * b + CW), V("oA")))
-        ts(V("di", 8, 16), V("sm", 11, 104, 13), 384.0, A.max)
-        ts(V("dj", 8, 16), V("di", 8, 16), 511, A.bitwise_and)
-        cp(V("oB"), V("dj", 8, 16))
-        for b in range(4):
-            for k in range(2):
-                tt(V("sa", 3 * b + k, 768, 12), ind(V("fh", CW * b, CW * b + CW), V("oB", 4 * k, 4 * k + 4)), V("ga", 128 * b + 64 * k, 128 * b + 64 * k + 64), A.add)
-        scan(V("sy"), V("sa"), V("sb"), -BIG, A.max, A.subtract)
-        cp(V("yt", 0, 256), V("sy", 1, 768, 3))
+        scores = V("sc", 15, 400, 16)
+        for f in range(2):
+            pm, o = ("pm1", "pm2")[f], 338 * f
+            scan(V(pm, 1, 26), V("rs25", 0, 25), V("s2", 0, 25) if f else scores, -NONE, A.min, A.max)
+            for x in range(2):
+                k = 2 * f + x
+                act(V("junk", 16 * k, 16 * k + 13), V(pm, 13 * x, 13 * x + 13), -1.0, F.Sign, V(pm, 13 * x + 12, 13 * x + 13), V("ix", k, k + 1))
+            for x in range(2):
+                ts(V("hm", o + 169 * x, o + 169 * x + 169), V("we", 0, 169), V("ix", 2 * f + x, 2 * f + x + 1), A.is_gt)
+            scan(V("kr", o, o + 338), V("hm", o, o + 338), V("df"), 0.0, A.mult, A.add)
+            row = V("kr", o + 12, o + 338, 13)
+            if f == 0:
+                ts(V("pen", 0, 25), V("kr", 25, 338, 13), 0.0, A.not_equal, -BIG, A.mult)
+                tt(V("s2", 0, 25), scores, V("pen", 0, 25), A.add)
+            a, p0, s0, k0 = 52 * f, (0, 156)[f], (52, 208)[f], (104, 130)[f]
+            tt(V("ka", a, a + 26), V("k2c"), row, A.subtract)
+            tt(V("ka", a + 26, a + 52), V("k2c"), row, A.add)
+            scan(V("ps", k0, k0 + 26), V("hm", o + 156, o + 182), V("dk"), 0.0, A.mult, A.add)
+            scan(V("ps", p0, p0 + 52), V("rsk"), V("ka", a, a + 52), -BIG, A.min, A.max)
+            scan(V("ps", s0 + 1, s0 + 52), V("ka", a + 1, a + 52), V("ps", p0, p0 + 51), V("nq", 0, 1), A.max, A.min)
+            ts(V("di", 10 * f, 10 * f + 10), V("ps", 130 * f + 12, 130 * f + 130, 13), Q, A.mult)
+            ts(V("dj", 10 * f, 10 * f + 10), V("di", 10 * f, 10 * f + 10), 511, A.bitwise_and)
+            la, lb, lk = (0, 2)[f], (4, 6)[f], (8, 0)[f]
+            for b in range(4):
+                ts(V("gl", 40 * f + 10 * b, 40 * f + 10 * b + 10), V("dj", 10 * f, 10 * f + 10), 4.0, A.mult, float(b), A.add)
+            for b in range(4):
+                c, e = 40 * f + 10 * b, 384 * f + 3 * b
+                h = 256 * f + 64 * b
+                act(V("ga", h, h + 64), ind(V("fx"), V("gl", c + la, c + la + 4)))
+                for k in range(2):
+                    tt(V("sa", e + k, 384 * f + 384, 12), ind(V("fx"), V("gl", c + lb + 2 * k, c + lb + 2 * k + 2)), V("ga", h + 32 * k, h + 32 * k + 32), A.add)
+            for b in range(4):
+                c, e = 40 * f + 10 * b, 384 * f + 3 * b
+                act(V("sb", e + 1, 384 * f + 384, 12), ind(V("fx"), V("gl", c + lk, c + lk + 2)), 2.0)
+            scan(V("sy", 384 * f, 384 * f + 384), V("sa", 384 * f, 384 * f + 384), V("sb", 384 * f, 384 * f + 384), -BIG, A.max, A.subtract)
+            ts(V("yt", 128 * f, 128 * f + 128), V("sy", 384 * f + 1, 384 * f + 384, 3), 0.5, A.mult)
         quant(V("yc%d" % t), V("yp%d" % t), V("yt"))
         src, dst, ca, cb = route(T, topo, rank)
-        sent = post([(dst if k is None else k, (out if k is None else mid) + str(t), mine + str(t), sem + str(t))
+        sent = post([(dst, out, 64 + 128 * t, mine + str(t), sem + str(t)) if k is None else (k, mid + str(t), 0, mine + str(t), sem + str(t))
                      for k, sem, mid, out, mine in ((ca, "ac", "rc", "lc", "yc"), (cb, "ap", "rp", "lp", "yp"))])
-        for f in range(2):
-            for x in range(2):
-                ts(V("oo", 26 * f + 13 * x, 26 * f + 13 * x + 13), V("it13"), V("ix", 2 * f + x, 2 * f + x + 1), A.is_equal, -2.0, A.mult)
-        ts(V("pp"), V("kk", 12, 728, 14), -1.0 / Q, A.mult, 0.0, A.max)
-        ts(V("nn"), V("kk", 12, 728, 14), 1.0 / Q, A.mult, 0.0, A.max)
         if t == 0:
-            ts(V("pd", 3, 4), pt, 26.0, A.mult, p4, A.add)
-            ts(V("pd", 4, 5), p1, -52.0, A.mult, 26.0, A.add)
-            tt(V("uX"), V("uX"), V("uC"), A.add)
-            ts(V("pd", 6, 7), pt, 26.0, A.mult, V("pd", 4, 5), A.add)
-            ts(V("LI"), V("uY"), V("pd", 3, 4), A.add)
-            ts(V("LJ"), V("uX"), V("pd", 6, 7), A.add)
-        tt(V("w", 26, 78), V("pp"), V("oo"), A.add)
-        for f in range(2):
-            tt(V("w", 78 * f, 78 * f + 26), V("nn", 26 * f, 26 * f + 26), V("oo", 26 * f, 26 * f + 26), A.add)
-        if t == 0:
-            fill(V("sg"), -1.0)
+            stream_lists()
             quant(V("zq"), V("zs"), V("zt"))
-            fill(V("sg", 0, 576, 4), 0.0)
-            fill(V("sg", 2, 576, 4), 1.0)
-            for k in range(R):
-                dma("y", u8(T, "lc%d" % k, 64, 128), u8(T, "zq", 64, 128), V("zq")[1], V("lc%d" % k, 64, 128)[1])
-                dma("y", u8(T, "lp%d" % k, 64, 128), u8(T, "zs", 64, 128), V("zs")[1], V("lp%d" % k, 64, 128)[1])
+            for k in range(R + 1):
+                dma("y", u8(T, "lc", 128 * k, 128 * k + 64), u8(T, "zq", 0, 64), V("zq")[1], V("lc", 128 * k, 128 * k + 64)[1])
+                dma("y", u8(T, "lp", 128 * k, 128 * k + 64), u8(T, "zs", 0, 64), V("zs")[1], V("lp", 128 * k, 128 * k + 64)[1])
+        rows = V("kr", 12, 676, 13)
+        ts(V("oo"), rows, MU, A.is_equal, -2.0, A.mult)
+        act(V("pp"), rows, 1.0, F.Relu)
+        act(V("nn"), rows, -1.0, F.Relu)
+        tt(V("w", 104, 130), V("kr", 12, 338, 13), V("kr", 350, 676, 13), A.add)
+        tt(V("w", 0, 52), V("pp"), V("oo"), A.add)
+        tt(V("w", 52, 104), V("nn"), V("oo"), A.add)
+        act(V("sta"), ind(V("w"), V("La")), 64.0, bias=192.0)
+        act(V("stb"), ind(V("w"), V("Lb")), 1.0 / 64)
         for b in range(4):
             act(V("y32", 64 * b, 64 * b + 64), V("yt", b, 256, 4), 32.0)
-        half = ((0, 18), (18, 36))
-        for a, b in half:
-            act(V("ei", 16 * a, 16 * b), ind(V("w"), V("LI", a, b)))
         for b in range(4):
-            act(V("fx", b, 1536, 4), V("fh", CW * b, CW * b + 384), 2.0)
-        for b in range(4):
-            ts(V("so", 4 * b, 4 * b + 4), V("kk", 181, 728, 182), 4.0, A.mult, 16384.0 + b, A.add)
-        for a, b in half:
-            tt(V("pr", 16 * a, 16 * b), ind(V("w"), V("LJ", a, b)), V("ei", 16 * a, 16 * b), A.mult)
+            ts(V("so", 4 * b, 4 * b + 4), V("dj", 8, 12), 4.0, A.mult, float(b), A.add)
+        for d in range(1, 7):
+            scan(V("pr", 120 * d - 120, 120 * d), V("sta", 0, 120), V("stb", 10 * d, 10 * d + 120), -BIG, A.max, A.mult)
         scan(V("s5"), V("sg"), V("pr"), 0.0, A.mult, A.add)
-        tt(V("sp"), V("s5", 3, 576, 4), V("pw"), A.add)
-        ts(V("pw"), V("sp"), -3.0, A.max, 3.0, A.min)
+        scan(V("sp"), V("s5", 4, 720, 5), V("bs"), -BIG, A.max, A.add)
+        ts(V("bs"), V("sp"), -SHIFT - 3.0, A.max, 3.0 - SHIFT, A.min)
+        act(V("win", 0, 144), V("bs"), bias=SHIFT)
+        act(V("win", 144, 288), V("bs"), -1.0, bias=-SHIFT)
         if t < R - 1:
-            penalties()
-            weights()
-            table_p()
-            table_b()
+            table()
         else:
-            act(V("win1", 0, 144), V("pw"))
-            act(V("win1", 144, 288), V("pw"), -1.0)
-            act(V("tb1"), ind(V("win1"), L0))
+            act(V("win", 288, 289), V("win", 289, 290))
+            act(V("tb"), ind(V("win"), V("LT")))
+            for e in range(12):
+                act(V("ob", e, 300, 12), V("tb", 14 + e, 338, 13), -1.0)
             for x in range(2):
-                for e in range(12):
-                    act(V("ob", 144 * x + e, 144 * x + 144, 12), V("tb1", 182 * x + e, 182 * x + 168, 14))
-            dma("y", T.oa[:], T.ob[:], V("ob")[1], [])
+                dma("y", T.oa[:, 144 * x:144 * x + 144], T.ob[:, 156 * x:156 * x + 144], V("ob")[1], [])
             quant(V("vq"), V("vs"), V("vt0"))
         sender, arr = route(T, topo, (rank - 1) % N), []
         for sem, k in (("ac%d" % t, sender[2]), ("ap%d" % t, sender[3])):
             arr.append((sem, len(topo.engines(sender[0] if k is None else k, core))))
-        for b in range(4):
-            mm(V("psE", 512 * b, 512 * b + 128), V("wq", 128 * b, 128 * b + 128), V("wp", 128 * b, 128 * b + 128), V("lc%d" % t), V("lp%d" % t), (sent, arr))
-        for b in range(4):
-            tt(V("vf", 64 * b, 64 * b + 64), V("psE", 512 * b, 512 * b + 64), V("y32", 64 * b, 64 * b + 64), A.add)
-            ts(V("vt", 64 * b, 64 * b + 64), V("vf", 64 * b, 64 * b + 64), 0.03125, A.mult)
-        run("v", lambda e: e.tensor_copy(T.fx[:, 0:1664].indirect(T.so[:, 0:16]), T.vt[:]), [V("vt"), V("so")], [V("fx")], 1000.0)
+        for h in range(2):
+            def pair(e, h=h, o=128 * t):
+                out, b = T.psE[:, 512 * h:512 * h + 128], 256 * h
+                e.matmul_mx(out, T.wq[:, b:b + 128], T.wp[:, b:b + 128], T.lc[:, o + 64:o + 192], T.lp[:, o + 64:o + 192], True, False)
+                return e.matmul_mx(out, T.wq[:, b + 128:b + 256], T.wp[:, b + 128:b + 256], T.lc[:, o:o + 128], T.lp[:, o:o + 128], False, True)
+            run("t", pair, [V("wq"), V("wp"), V("lc"), V("lp")], [V("psE", 512 * h, 512 * h + 128)], 370.0, (sent, arr, NEAR if direct == (t % 2 == 0) else FAR))
+        for h in range(2):
+            tt(V("v32", 128 * h, 128 * h + 128), V("psE", 512 * h, 512 * h + 128), V("y32", 128 * h, 128 * h + 128), A.add)
+            ts(V("vt", 128 * h, 128 * h + 128), V("v32", 128 * h, 128 * h + 128), 0.03125, A.mult)
+        run("v", lambda e: e.tensor_copy(T.fx[:, 0:1664].indirect(T.so[:, 0:16]), T.vt[:]), [V("vt"), V("so")], [V("fx")], 1060.0)
+        if t < R - 1:
+            iota(V("fx", 1536, 1664), [[0, 128]])
 
     score_products(V("vq"), V("vs"))
-    dma("y", T.oc[:], u8(T, "xq", 0, 384), V("xq")[1], [])
-    for k in range(4):
-        dma("y", T.osc[4 * k:4 * k + 4, :], T.xs[32 * k:32 * k + 4, :], V("xs")[1], [])
     for k in range(3):
-        cp(V("ysb", 128 * k, 128 * k + 128), V("psP", 512 * k, 512 * k + 128))
-    dma("s", T.y[:], T.ysb[:], V("ysb")[1], [])
+        a = 128 * k
+        dma("y", T.oc[:, 4 * a:4 * a + 512], u8(T, "xq", a, a + 128), V("xq", a, a + 128)[1], [])
+        (cp if k == 2 else act)(V("ysb", a, a + 128), V("psP", 512 * k, 512 * k + 128))
+        dma("sys"[k], T.y[:, a:a + 128], T.ysb[:, a:a + 128], V("ysb", a, a + 128)[1], [])
+    for k in range(4):
+        dma("ys"[k % 2], T.osc[4 * k:4 * k + 4, :], T.xs[32 * k:32 * k + 4, :], V("xs")[1], [], 2000.0)
     issue()
     for sem in count:
         need("g", sem, count[sem], {})

@@ -6,7 +6,8 @@ NONE = 2.0 ** 79
 Q = 16384.0
 MU = 1.0 / 64
 SHIFT = 192.0
-WAKE, NEAR, FAR = 110.0, 2600.0, 5600.0
+CASES = ((50.0, 180.0, 25.0, (1100.0, 2400.0), (800.0, 1600.0), 0.7, 1.0), (50.0, 60.0, 20.0, (1900.0, 4000.0), (400.0, 800.0), 1.0, 1.0))
+PLAN, TRIES = {}, 32000
 SCRATCH, CODES = {}, set()
 
 
@@ -20,16 +21,17 @@ def declare(dtype, spec):
 
 
 declare("bfloat16", "fx:1664 ut:512 vt0:512 yt:512 zt:512 et:520 ones:128 ga:512 sa:768 sb:768 sy:768 y32:256 v32:256 vt:256 "
-        "hm:676 we:170 tb:352 df:338 kr:676 win:304 bs:144 sp:144 pr:720 s5:720 sg:720 sta:128 stb:192 w:192 pp:52 nn:52 oo:52 "
-        "iC:400 cap:400 rs2:400")
+        "hm:676 we:170 tb:704 df:676 alt:338 kr:676 win:304 bs:144 sp:144 pr:720 s5:720 sg:720 sta:128 stb:192 w:192 pp:130 oo:130 "
+        "iC:400 cap:400 rs2:400 rsk:104")
 declare("float8_e4m3fn_x4", "uq:128 urq:128 vq:128 eq:512 zq:128 wq:512 xq:384 lc:448 " + " ".join("yc%d:128 rc%d:64" % (t, t) for t in range(R)))
 declare("uint8", "us:128 urs:128 vs:128 es:512 zs:128 wp:512 xs:384 lp:448 " + " ".join("yp%d:128 rp%d:64" % (t, t) for t in range(R)))
-declare("float32", "psP:1536 psE:2048 psc:416 gm:400 sc:400 pm1:26 pm2:26 pen:26 s2:26 rs25:26 ix:4 junk:64 ka:104 ps:260 rsk:52 "
-        "k2i:26 k2c:26 nlf:28 nq:28 dk:26 ob:300 ysb:384 rt:384 iK:384 pf:4 pd:4 "
-        "lm:22 lA:22 lB:22 lC:22 lD:22 lE:22 lF:22 lG:22 lH:22 uA:9 uB:9 uC:9 uD:9 uE:9 "
-        "mA:12 mB:12 mC:12 mD:24 mE:12 mF:12")
-declare("int32", "di:20 dj:20 ndi:24 ari:288 pI:4 pA:4 ui:8 li:22 mi:12 mj:24")
-declare("uint16", "gl:80 so:16 nd16:24 nl:26 ul:8 LT:22 LP:10 La:8 Lb:12")
+declare("float32", "psP:1536 psE:2048 psc:416 gm:400 sc:400 pm1:26 pm2:26 pen:26 s2:26 rs25:26 ix:4 signs:64 ka:104 ps:260 "
+        "k2i:26 k2c:52 nlf:28 nq:28 dk:26 ob:304 ysb:384 rt:384 iK:384 pf:4 pd:4 few:504")
+PART = {}
+for item in "lm:22 lA:22 lB:22 lC:22 lD:22 lE:22 lF:22 lG:22 lH:22 lI:22 uA:9 uB:9 uC:9 uD:9 uE:9 mA:12 mB:12 mC:12 mD:24 mE:12 mF:12".split():
+    PART[item[:2]] = (24 * len(PART), int(item[3:]))
+declare("int32", "di:16 dj:16 lo:20 ndi:24 ari:296 pI:4 pA:4 ui:8 li:22 mi:12 mj:24")
+declare("uint16", "gl:80 LP:10 LO:20 so:16 nd16:24 nl:26 ul:8 LT:22 L0:22 La:8 Lb:12")
 DMAS = 34
 SEMAPHORES = ["qv", "qs", "qt", "qg", "sent"] + ["d%d" % i for i in range(DMAS)] + ["ac%d" % t for t in range(R)] + ["ap%d" % t for t in range(R)]
 
@@ -67,6 +69,135 @@ def relay_program(g, core, T, topo):
         g.wait_ge(T.sem.sent, total)
 
 
+def plan(first, second):
+    n, ops = len(first), first + second
+    m = len(ops)
+    names = {}
+    line = [names.setdefault((ops[k][0], k < n), len(names)) for k in range(m)]
+    marks = [k for k in range(m) if ops[k][3] == "sent"]
+    graphs = []
+    for wake, across, more, way, once, by, speed in CASES:
+        cost = [o[2] * by if o[4] == 16 else o[2] * speed + more for o in ops]
+        busy = [90.0 if ops[k][4] == 16 else cost[k] for k in range(m)]
+        before = [[] for _ in range(m)]
+        for k in range(m):
+            side = int(k >= n)
+            before[k] += [(side * n + d, busy[side * n + d]) for d in ops[k][7]]
+            for d in ops[k][5]:
+                d += side * n
+                before[k].append((d, cost[d] + (0.0 if d in marks else wake if ops[d][0] == ops[k][0] and ops[d][4] == 1 else across)))
+                if ops[k][6] and d in marks:
+                    t = marks.index(d) % R
+                    before[k].append((marks[t + R * (1 - side)], way[side] + (0.0 if t else once[side])))
+        graphs.append((cost, busy, before))
+    cost, busy, before = graphs[0]
+    behind = [[] for _ in range(m)]
+    for k in range(m):
+        for d, c in before[k]:
+            behind[d].append((k, c))
+    tails = [k for k in range(m) if not behind[k]]
+
+    def times(order, a=0, seen=None):
+        value, out, who0 = 0.0, [], [-1] * len(names)
+        for k in order[:a]:
+            who0[line[k]] = k
+        rest = order[a:]
+        for i, (cost, busy, before) in enumerate(graphs):
+            start, ahead = (list(seen[i][0]), list(seen[i][1])) if seen else ([0.0] * m, [-1] * m)
+            who = list(who0)
+            end = [start[k] + busy[k] if k >= 0 else 0.0 for k in who]
+            for k in rest:
+                q = line[k]
+                t = end[q]
+                for d, c in before[k]:
+                    x = start[d] + c
+                    if x > t:
+                        t = x
+                start[k], end[q], ahead[k], who[q] = t, t + busy[k], who[q], k
+            value += max(start[k] + cost[k] for k in tails) + 0.01 * sum(start[k] for k in marks)
+            out.append((start, ahead))
+        return value / len(graphs), out
+
+    left, back = [len(e) for e in behind], list(tails)
+    for k in back:
+        for d, c in before[k]:
+            left[d] -= 1
+            if not left[d]:
+                back.append(d)
+    far = [0.0] * m
+    for k in back:
+        far[k] = max([far[u] + c for u, c in behind[k]] + [cost[k]])
+    start, taken = [0.0] * m, [[] for _ in names]
+    for k in sorted(range(m), key=lambda k: -far[k]):
+        t0, at = max([start[d] + c for d, c in before[k]] or [0.0]), 0
+        for a, b in taken[line[k]]:
+            if t0 + busy[k] <= a:
+                break
+            t0, at = max(t0, b), at + 1
+        taken[line[k]].insert(at, (t0, t0 + busy[k]))
+        start[k] = t0
+    order = sorted(range(m), key=lambda k: (start[k], -far[k]))
+    value, seen = times(order)
+    best, seed = (value, order), [20261]
+
+    def draw(count):
+        seed[0] = (seed[0] * 1103515245 + 12345) % 2147483648
+        return (seed[0] >> 8) % count
+
+    where = [0] * m
+    for i, u in enumerate(order):
+        where[u] = i
+    for trial in range(TRIES):
+        case = draw(len(graphs))
+        (cost, busy, before), (start, ahead) = graphs[case], seen[case]
+        k = marks[draw(len(marks))] if draw(10) < 3 else max(tails, key=lambda k: start[k] + cost[k])
+        held = []
+        while start[k] > 0.0:
+            d, x = -1, -1.0
+            for e, c in before[k]:
+                if start[e] + c > x:
+                    d, x = e, start[e] + c
+            if x < start[k] - 0.01:
+                held.append((k, ahead[k]))
+                k = ahead[k]
+            else:
+                if ahead[k] >= 0 and draw(10) == 0:
+                    held.append((k, ahead[k]))
+                k = d
+        if not held:
+            continue
+        k, j = held[draw(len(held))]
+        if draw(2):
+            for _ in range((0, 0, 1, 2, 4, 8, 20)[draw(7)]):
+                if ahead[j] >= 0:
+                    j = ahead[j]
+            move, todo, a, b = {k}, [k], where[j], where[k] + 1
+            while todo:
+                for d, c in before[todo.pop()]:
+                    if where[d] >= a and d not in move:
+                        move.add(d)
+                        todo.append(d)
+            if j in move:
+                continue
+            new = order[:a] + [u for u in order[a:b] if u in move] + [u for u in order[a:b] if u not in move] + order[b:]
+        else:
+            move, todo, a, b = {j}, [j], where[j], min(m, where[k] + 1 + (0, 0, 5, 20, 60, 150)[draw(6)])
+            while todo:
+                for u, c in behind[todo.pop()]:
+                    if where[u] < b and u not in move:
+                        move.add(u)
+                        todo.append(u)
+            new = order[:a] + [u for u in order[a:b] if u not in move] + [u for u in order[a:b] if u in move] + order[b:]
+        v, s = times(new, a, seen)
+        if v <= value + 0.2 * draw(1000) * (1.0 - trial / TRIES) ** 2:
+            order, value, seen = sorted(new, key=lambda k: s[0][0][k]), v, s
+            for i, u in enumerate(order):
+                where[u] = i
+            if v < best[0]:
+                best = (v, new)
+    return [k for k in best[1] if k < n], [k - n for k in best[1] if k >= n]
+
+
 def overlap(a, b):
     if a[0] != b[0] or a[1] >= b[2] or b[1] >= a[2]:
         return False
@@ -78,74 +209,57 @@ def rank_program(g, core, T, topo):
     if rank is None:
         relay_program(g, core, T, topo)
         return
+    if not PLAN:
+        PLAN[True], PLAN[False] = plan(calls(g, core, T, topo, True, False), calls(g, core, T, topo, False, False))
+    calls(g, core, T, topo, route(T, topo, (rank - 1) % N)[2] is None, True)
+
+
+def calls(g, core, T, topo, direct, go):
+    rank = T.rank_of(core)
     A = AluOpType
     F = ActivationFunctionType
     queue = {"v": g.vector, "s": g.scalar, "t": g.tensor, "g": g, "y": g.sync}
     count = {}
     known = {k: {} for k in queue}
-    direct = route(T, topo, (rank - 1) % N)[2] is None
     free = ["d%d" % i for i in range(DMAS)]
     ops, last = [], {}
 
-    def add(q, call, reads, writes, cost, sem=None, inc=1, after=(), arrivals=(), lag=0.0):
+    def add(q, call, reads, writes, cost, sem=None, inc=1, after=(), arrivals=()):
         k = len(ops)
-        deps = {d: lag for d in after}
+        deps = set(after)
         for kind, regions in (("r", reads), ("w", writes)):
             for x in regions:
                 for o, y, d in last.get(x[0], []):
                     if (kind == "w" or o == "w" or x[0] in ("psP", "psE") and ops[d][0] != q) and overlap(x, y):
-                        deps.setdefault(d, 0.0)
+                        deps.add(d)
         for x in writes:
             last[x[0]] = [e for e in last.get(x[0], []) if not (e[1][1] >= x[1] and e[1][2] <= x[2] and x[3] == 1)]
         for kind, regions in (("r", reads), ("w", writes)):
             for x in regions:
                 last.setdefault(x[0], []).append((kind, x, k))
-        ops.append((q, call, cost, sem or "q" + q, inc, deps, arrivals))
+        ops.append((q, call, cost, sem or "q" + q, inc, sorted(deps), arrivals, []))
         return k
 
     def run(q, call, reads, writes, cost, arr=None):
         bank = lambda x: (x[0], x[1] // 512 * 512, x[1] // 512 * 512 + 512, 1) if x[0] in ("psP", "psE") else x
         reads = [bank(x) for o in reads for x in o[1]]
         writes = [bank(x) for o in writes for x in o[1]]
-        add(q, lambda e: call(e).then_inc(T.sem["q" + q], 1), reads, writes, cost,
-            after=[arr[0]] if arr else (), arrivals=arr[1] if arr else (), lag=arr[2] if arr else 0.0)
+        add(q, lambda e: call(e).then_inc(T.sem["q" + q], 1), reads, writes, cost, after=[arr[0]] if arr else (), arrivals=arr[1] if arr else ())
 
-    def dma(q, out, in_, reads, writes, cost=2400.0):
+    def dma(q, out, in_, reads, writes, cost=2400.0, after=()):
         sem = free.pop(0)
-        add(q, lambda e: e.dma_start(out, in_).then_inc(T.sem[sem], 16), reads, writes, cost, sem, 16)
+        add(q, lambda e: e.dma_start(out, in_).then_inc(T.sem[sem], 16), reads, writes, cost, sem, 16, after)
 
     def post(writes):
         def call(e):
             for to, out, at, mine, sem in writes:
                 count["sent"] = count.get("sent", 0) + send(e, T, topo, core, to, out, at, mine, sem)
-        return add("g", call, [(w[3], 0, 128, 1) for w in writes], [], 1400.0, "sent", 0)
+        return add("g", call, [(w[3], 0, 128, 1) for w in writes], [], 600.0, "sent", 0)
 
     def issue():
-        n = len(ops)
-        users = [[] for _ in range(n)]
-        far = [0.0] * n
-        for k in range(n):
-            for d in ops[k][5]:
-                users[d].append(k)
-        for k in range(n - 1, -1, -1):
-            far[k] = ops[k][2] + max([far[u] + WAKE + ops[u][5][k] for u in users[k]] or [0.0])
-        line = {q: [] for q in queue}
-        start = [0.0] * n
-        for k in sorted(range(n), key=lambda k: (-far[k], k)):
-            q, cost, deps = ops[k][0], ops[k][2], ops[k][5]
-            t0 = max([start[d] + ops[d][2] + WAKE + deps[d] for d in deps] or [0.0])
-            busy = 60.0 if ops[k][4] == 16 else cost
-            at = 0
-            for a, b in line[q]:
-                if t0 + busy <= a:
-                    break
-                t0 = max(t0, b)
-                at += 1
-            line[q].insert(at, (t0, t0 + busy))
-            start[k] = t0
-        mark = [None] * n
-        for k in sorted(range(n), key=lambda k: (start[k], -far[k], k)):
-            q, call, cost, sem, inc, deps, arrivals = ops[k]
+        mark = [None] * len(ops)
+        for k in PLAN[direct]:
+            q, call, cost, sem, inc, deps, arrivals = ops[k][:7]
             for d in sorted(deps, key=lambda d: -mark[d][1]):
                 if mark[d][0] != "sent":
                     need(q, *mark[d])
@@ -165,6 +279,8 @@ def rank_program(g, core, T, topo):
                 known[q][s] = max(known[q].get(s, 0), clock[s])
 
     def V(name, a=0, b=None, step=1):
+        if name in PART:
+            name, a, b = "few", PART[name][0] + a, PART[name][0] + (PART[name][1] if b is None else b)
         b = SCRATCH[name][1][1] if b is None else b
         return (T[name][:, a:b:step] if step > 1 else T[name][:, a:b], [(name, a, b, step)])
 
@@ -181,8 +297,10 @@ def rank_program(g, core, T, topo):
         name, a, b, step = v[1][0]
         return (b - a + step - 1) // step
 
-    def fast(n, *v):
-        return max(66, 1.04 * n * (0.5 if all(SCRATCH[x[1][0][0]][2] in ("bfloat16", "uint16") for x in v) else 1))
+    def fast(out, *v):
+        if len(v[0]) > 2:
+            return 50 + 1.62 * size(out)
+        return max(66, 1.04 * size(out) * (0.5 if all(SCRATCH[x[1][0][0]][2] in ("bfloat16", "uint16") for x in v + (out,)) else 1))
 
     def tt(out, a, b, op):
         n = size(out)
@@ -191,24 +309,27 @@ def rank_program(g, core, T, topo):
 
     def ts(out, a, s1, op0, s2=None, op1=None):
         if op1 is None:
-            run("v", lambda e: e.tensor_scalar(out[0], a[0], val(s1), None, op0), [a] + reg(s1), [out], fast(size(out), a, out))
+            run("v", lambda e: e.tensor_scalar(out[0], a[0], val(s1), None, op0), [a] + reg(s1), [out], fast(out, a))
         else:
-            run("v", lambda e: e.tensor_scalar(out[0], a[0], val(s1), val(s2), op0, op1), [a] + reg(s1, s2), [out], fast(size(out), a, out))
+            run("v", lambda e: e.tensor_scalar(out[0], a[0], val(s1), val(s2), op0, op1), [a] + reg(s1, s2), [out], fast(out, a))
 
     def cp(out, a):
-        run("v", lambda e: e.tensor_copy(out[0], a[0]), [a], [out], fast(size(out), a, out))
+        run("v", lambda e: e.tensor_copy(out[0], a[0]), [a], [out], fast(out, a))
+
+    def scatter(win, off, a):
+        run("v", lambda e: e.tensor_copy(win[0].indirect(off[0]), a[0]), [a, off], [win], 50 + 3.94 * size(a))
 
     def scan(out, d0, d1, initial, op0, op1):
-        run("v", lambda e: e.tensor_tensor_scan(out[0], d0[0], d1[0], val(initial), op0, op1), [d0, d1] + reg(initial), [out], fast(size(out), d0, d1, out))
+        run("v", lambda e: e.tensor_tensor_scan(out[0], d0[0], d1[0], initial, op0, op1), [d0, d1], [out], fast(out, d0, d1))
 
     def fill(out, c):
-        run("v", lambda e: e.memset(out[0], c), [], [out], fast(size(out), out))
+        run("v", lambda e: e.memset(out[0], c), [], [out], fast(out, out))
 
     def quant(q, s, t):
         run("v", lambda e: e.quantize_mx(q[0], s[0], t[0]), [t], [q, s], 15 + 0.275 * size(t))
 
     def mm(out, w, ws, x, xs):
-        run("t", lambda e: e.matmul_mx(out[0], w[0], ws[0], x[0], xs[0], True, True), [w, ws, x, xs], [out], 1.3 * size(x) + 20)
+        run("t", lambda e: e.matmul_mx(out[0], w[0], ws[0], x[0], xs[0], True, True), [w, ws, x, xs], [out], 1.4 * size(x) + 23)
 
     def act(out, a, scale=1.0, func=None, bias=None, accum=None):
         kw = {}
@@ -223,7 +344,7 @@ def rank_program(g, core, T, topo):
             65 + 1.62 * size(out) if len(a) > 2 else max(66, 1.04 * size(out)) + (20 if accum is not None else 0))
 
     def iota(out, pattern, base=0, cm=0):
-        cost = 130 + 2.1 * size(out)
+        cost = 130 + 2.1 * (out[1][0][2] - out[1][0][1])
         if SCRATCH[out[1][0][0]][2] == "int32":
             run("g", lambda e: e.iota(out[0], pattern, base, cm), [], [out], cost)
         else:
@@ -233,40 +354,51 @@ def rank_program(g, core, T, topo):
     dma("s", T.ut[:], T.u[:], [], V("ut")[1], 2800.0)
     for k, q in enumerate("ysy"):
         dma(q, T.fx[:, 512 * k:512 * k + 512], T.x[:, 512 * k:512 * k + 512], [], V("fx", 512 * k, 512 * k + 512)[1], 2900.0 + 300 * k)
-    dma("s", T.ari[:], T.ar[:], [], V("ari")[1], 4000.0)
+    dma("s", T.ari[:, 0:288], T.ar[:], [], V("ari", 0, 288)[1], 3300.0)
+    for a, b in ((0, 2), (2, 4), (1, 3), (3, 5)):
+        ops[b][7].append(a)
 
     iota(V("pI"), [[0, 4]], 0, 1)
+    iota(V("lm"), [[16, 22]])
     iota(V("iK"), [[1, 384]])
     iota(V("ui"), [[16, 8]])
-    iota(V("lm"), [[16, 22]])
+    iota(V("ari", 288, 296), [[0, 8]])
+    fill(V("ones"), 1.0)
+    one = lambda n: V("ones", 0, n)
+    for k in range(0, 520, 104):
+        act(V("et", k, k + 104), one(104), 0.0)
+    run("g", lambda e: e.affine_select(T.et[:, 3:515:4], T.ones[:], [[-1, 128]], A.is_equal, 0.0, 0, 1), [V("ones")], [V("et")], 900.0)
+    iota(V("iC"), [[0, 25], [1, 16]])
     iota(V("uA"), [[0, 3], [8, 3]])
     iota(V("uB"), [[2, 3], [0, 3]], 1)
-    iota(V("iC"), [[0, 25], [1, 16]])
-    fill(V("ones"), 1.0)
-    fill(V("et"), 0.0)
-    run("g", lambda e: e.affine_select(T.et[:, 3:515:4], T.ones[:], [[-1, 128]], A.is_equal, 0.0, 0, 1), [V("ones")], [V("et")], 440.0)
-    iota(V("k2i"), [[0, 2], [-512, 13]], int(512 * 13 - Q))
-    iota(V("k2i", 0, 26, 13), [[0, 2]])
+    iota(V("alt"), [[0, 169], [1, 2]])
     iota(V("we", 0, 169), [[0, 13], [1, 13]])
-    iota(V("psc", 384, 416), [[0, 32]])
-    iota(V("fx", 1536, 1664), [[0, 128]])
-    iota(V("yt", 256, 512), [[0, 256]])
-    iota(V("sb", 0, 768, 3), [[0, 256]])
-    iota(V("zt"), [[0, 512]])
-    iota(V("w"), [[0, 192]])
+    iota(V("k2i"), [[0, 2], [-512, 13]], int(512 * 13 - Q))
     iota(V("win", 288, 304), [[0, 16]])
-    act(V("win", 288, 289), V("win", 289, 290), bias=MU)
-    iota(V("sg"), [[0, 720]], 1)
+    fill(V("rs2"), 0.0)
+    iota(V("fx", 1536, 1664), [[0, 128]])
+    iota(V("w"), [[0, 192]], -16)
     iota(V("sg", 0, 720, 5), [[0, 144]])
     iota(V("sg", 3, 720, 5), [[0, 144]], -1)
-    act(V("sa", 2, 768, 3), V("iC", 0, 256), 0.0, bias=-BIG)
-    act(V("sb", 2, 768, 3), V("iC", 0, 256), 0.0, bias=BIG)
-    act(V("rs25"), V("iC", 0, 26), 0.0, bias=BIG)
-    act(V("rs25", 12, 13), V("iC", 0, 1), 0.0, bias=-NONE)
-    act(V("rsk"), V("iC", 0, 52), 0.0, bias=BIG)
-    act(V("rsk", 0, 52, 13), V("iC", 0, 4), 0.0, bias=-BIG)
+    for k in (1, 2, 4):
+        fill(V("sg", k, 720, 5), 1.0)
+    fill(V("zt"), 0.0)
+    fill(V("yt", 256, 512), 0.0)
+    fill(V("sb", 0, 768, 3), 0.0)
+    early = [k for k in range(len(ops)) if ops[k][0] == "g"]
+    for a, b in zip(early, early[1:]):
+        ops[b][7].append(a)
+    act(V("win", 288, 289), one(1), MU)
+    act(V("psc", 384, 416), one(32), -BIG)
+    for h in range(2):
+        act(V("sa", 2 + 384 * h, 384 + 384 * h, 3), one(128), -BIG)
+        act(V("sb", 2 + 384 * h, 384 + 384 * h, 3), one(128), BIG)
+    act(V("rs25"), one(26), BIG)
+    act(V("rs25", 12, 13), one(1), -NONE)
+    act(V("rsk"), one(104), BIG)
+    act(V("rsk", 0, 104, 13), one(8), -BIG)
     for n in ("pm1", "pm2"):
-        act(V(n, 0, 1), V("iC", 0, 1), 0.0, bias=-NONE)
+        act(V(n, 0, 1), one(1), -NONE)
     act(V("k2i"), V("k2i"), 1.0 / Q)
 
     ts(V("pA", 0, 1), V("pI", 0, 1), 15, A.bitwise_and)
@@ -276,7 +408,8 @@ def rank_program(g, core, T, topo):
     p16, p8, p1 = (V("pf", k, k + 1) for k in range(3))
     for k, c in ((0, 384.0), (13, 400.0)):
         act(V("nlf", k, k + 1), p16, bias=c)
-    act(V("nlf", 26, 28), V("pf", 0, 2), 0.0)
+    act(V("nlf", 26, 28), one(2), 0.0)
+    beside = [len(ops) - 3, len(ops) - 2, len(ops) - 1]
     act(V("pd", 0, 1), p1, 144.0)
 
     def score_products(w, ws):
@@ -290,19 +423,18 @@ def rank_program(g, core, T, topo):
             mm(V("psE", 512 * b, 512 * b + 384), V("eq", 128 * b, 128 * b + 128), V("es", 128 * b, 128 * b + 128), V("xq"), V("xs"))
 
     cp(V("nd16"), V("ndi"))
-    act(V("rt"), ind(V("iK"), V("nd16")))
+    act(V("rt", 0, 192), ind(V("iK"), V("nd16", 0, 12)))
+    cp(V("rt", 192, 384), ind(V("iK"), V("nd16", 12, 24)))
     for x in range(2):
-        dma("ys"[x], T.nlf[:, 13 * x + 1:13 * x + 13], T.rt[0:128:16, 192 * x:192 * x + 192], V("rt")[1] + [("nlf", 0, 28, 13)],
-            [("nlf", 13 * x + 1, 13 * x + 13, 1)], 2100.0)
+        dma("y", T.nlf[:, 13 * x + 1:13 * x + 13], T.rt[0:128:16, 192 * x:192 * x + 192], V("rt", 192 * x, 192 * x + 192)[1],
+            [("nlf", 13 * x + 1, 13 * x + 13, 1)], 2100.0, beside)
     dma("y", T.wq[:, 0:512].bitcast(dt.uint8), T.wc[:], V("nlf")[1], V("wq")[1], 4000.0)
     dma("y", T.wp[:], T.ws[:], V("nlf")[1], V("wp")[1])
     dma("y", T.vt0[:], T.v[:], V("nlf")[1], V("vt0")[1])
-    act(V("cap"), V("iC"), -1.0, F.Square, p16)
-    ts(V("cap"), V("cap"), -2.0 * BIG, A.mult, BIG, A.add)
-    fill(V("cap", 192, 208), -BIG)
-    fill(V("rs2"), BIG)
+    ts(V("cap"), V("iC"), p16, A.not_equal, -BIG, A.mult)
+    act(V("cap", 192, 208), one(16), -BIG)
     cp(V("ul"), V("ui"))
-    fill(V("rs2", 0, 400, 16), -BIG)
+    act(V("rs2", 0, 400, 16), one(25), -BIG)
     quant(V("uq"), V("us"), V("ut"))
     run("v", lambda e: e.tensor_copy(T.urq[:, 0:128].bitcast(dt.uint32), T.uq[:, 0:128].bitcast(dt.uint32).indirect(T.ul[:, 0:8])),
         [V("uq"), V("ul")], [V("urq")], 260.0)
@@ -311,13 +443,15 @@ def rank_program(g, core, T, topo):
         quant(V("eq", 128 * b, 128 * b + 128), V("es", 128 * b, 128 * b + 128), V("et", 3 - b, 515 - b))
     cp(V("nl", 0, 25), V("nlf", 1, 26))
     act(V("nq"), V("nlf"), 1.0 / Q)
-    tt(V("k2c"), V("nq", 0, 26), V("k2i"), A.add)
+    tt(V("k2c", 0, 26), V("nq", 0, 26), V("k2i"), A.add)
+    act(V("k2c", 0, 26, 13), one(2), 384.0 / Q)
+    act(V("k2c", 26, 52), V("k2c", 0, 26))
     tt(V("dk"), V("nq", 0, 26), V("nq", 1, 27), A.subtract)
     act(V("dk", 12, 13), V("nq", 12, 13))
 
-    act(V("uA"), V("uA"), bias=p8)
+    ts(V("uA"), V("uA"), p8, A.add)
     ts(V("uC"), V("uA"), 12.0, A.is_ge)
-    act(V("uD"), V("uC"), -12.0)
+    ts(V("uD"), V("uA"), 12.0, A.is_ge, -12.0, A.mult)
     tt(V("uB"), V("uB"), V("uC"), A.add)
     tt(V("uA"), V("uA"), V("uD"), A.add)
     tt(V("uB"), V("uB"), V("uA"), A.add)
@@ -326,28 +460,31 @@ def rank_program(g, core, T, topo):
     tt(V("uE"), V("uE"), V("uB"), A.add)
     tt(V("uE"), V("uE"), V("uC"), A.add)
     cp(V("LP", 0, 9), V("uE"))
-    act(V("win", 0, 144), ind(V("ari"), V("LP", 0, 9)))
-    act(V("win", 144, 288), V("win", 0, 144), -1.0)
-    act(V("bs"), V("win", 0, 144), bias=-SHIFT)
+    act(V("bs"), ind(V("ari"), V("LP", 0, 9)), bias=-SHIFT)
 
-    act(V("lm"), V("lm"), bias=p16)
+    ts(V("lm"), V("lm"), p16, A.add)
     ts(V("li"), V("lm"), 1.0 / 13, A.mult, -6.0 / 13, A.add)
     ts(V("lB"), V("lm"), 169.0, A.is_ge)
-    cp(V("lA"), V("li"))
-    act(V("lC"), V("lB"), -13.0)
-    act(V("lD"), V("lA"), -13.0)
-    tt(V("lA"), V("lA"), V("lC"), A.add)
+    ts(V("lC"), V("lm"), 169.0, A.is_ge, -13.0, A.mult)
+    ts(V("lD"), V("li"), -13.0, A.mult)
+    tt(V("lA"), V("li"), V("lC"), A.add)
     tt(V("lD"), V("lD"), V("lm"), A.add)
-    tt(V("lC"), V("lA"), V("lD"), A.subtract)
     tt(V("lH"), V("lA"), V("lD"), A.mult)
+    ts(V("lI"), V("lD"), 12.0, A.mult, -13.0, A.add)
+    ts(V("lE"), V("lm"), 169.0, A.is_ge, 144.0, A.mult)
+    ts(V("lH"), V("lH"), 0.0, A.is_equal, 289.0, A.mult)
+    tt(V("lI"), V("lI"), V("lA"), A.add)
+    tt(V("lI"), V("lI"), V("lE"), A.add)
+    tt(V("lI"), V("lI"), V("lH"), A.max)
+    ts(V("L0"), V("lI"), 289.0, A.min)
+    tt(V("lC"), V("lA"), V("lD"), A.subtract)
     ts(V("lE"), V("lC"), 0.0, A.is_lt, 12.0, A.mult)
     act(V("lD"), V("lD"), 2.0, bias=-26.0)
     act(V("lA"), V("lA"), 2.0, bias=406.0)
     tt(V("lC"), V("lC"), V("lE"), A.add)
-    ts(V("lH"), V("lH"), 0.0, A.is_equal, 289.0, A.mult)
     act(V("lE"), V("lC"), 24.0)
-    ts(V("lF"), V("lC"), 7.0, A.is_ge, 1000.0, A.mult)
-    ts(V("lG"), V("lC"), 0.0, A.is_equal, 288.0, A.mult)
+    act(V("lF"), V("lC"), 1000.0, F.Relu, -6000.0)
+    act(V("lG"), V("lC"), -288.0, F.Relu, 288.0)
     tt(V("lD"), V("lD"), V("lE"), A.add)
     tt(V("lA"), V("lA"), V("lE"), A.subtract)
     tt(V("lD"), V("lD"), V("lF"), A.add)
@@ -357,12 +494,14 @@ def rank_program(g, core, T, topo):
     tt(V("lD"), V("lD"), V("lG"), A.max)
     ts(V("LT"), V("lD"), 289.0, A.min)
 
-    def table():
-        act(V("tb"), ind(V("win"), V("LT")))
-        for a, b in ((0, 84), (84, 169), (169, 253), (253, 338)):
-            tt(V("df", a, b), V("tb", a, b), V("tb", a + 1, b + 1), A.subtract)
-
-    table()
+    def table(first=False):
+        act(V("tb", 0, 704, 2), ind(V("ari"), V("L0")) if first else ind(V("win"), V("LT")))
+        if first:
+            for x in range(2):
+                act(V("tb", 338 * x + 28, 338 * x + 338, 28), one(12), MU)
+        for a in (0, 338):
+            act(V("tb", a + 1, a + 338, 2), V("tb", a + 2, a + 340, 2), -1.0)
+            scan(V("df", a, a + 338), V("alt"), V("tb", a, a + 338), 0.0, A.mult, A.add)
 
     def stream_lists():
         m = V("lm", 0, 12)
@@ -385,52 +524,50 @@ def rank_program(g, core, T, topo):
         tt(V("mF"), V("mF"), V("mC"), A.add)
         ts(V("La"), V("mF", 0, 8), 52.0, A.add)
 
+    table(True)
+
     for t in range(R):
         score_products(V("urq"), V("urs"))
         unpack_products()
         for k in range(3):
-            cp(V("psc", 128 * k, 128 * k + 128), V("psP", 512 * k, 512 * k + 128))
+            (cp if k else act)(V("psc", 128 * k, 128 * k + 128), V("psP", 512 * k, 512 * k + 128))
         for b in range(4):
             for h in range(2):
                 act(V("fx", b + 768 * h, 768 * h + 768, 4), V("psE", 512 * b + 192 * h, 512 * b + 192 * h + 192))
-        tt(V("gm"), ind(V("psc"), V("nl", 0, 25)), V("cap"), A.min)
-        scan(V("sc"), V("rs2"), V("gm"), -BIG, A.min, A.max)
+        tt(V("gm"), ind(V("psc"), V("nl", 0, 25)), V("cap"), A.add)
+        scan(V("sc"), V("rs2"), V("gm"), 0.0, A.add, A.max)
         scores = V("sc", 15, 400, 16)
         for f in range(2):
             pm, o = ("pm1", "pm2")[f], 338 * f
             scan(V(pm, 1, 26), V("rs25", 0, 25), V("s2", 0, 25) if f else scores, -NONE, A.min, A.max)
             for x in range(2):
                 k = 2 * f + x
-                act(V("junk", 16 * k, 16 * k + 13), V(pm, 13 * x, 13 * x + 13), -1.0, F.Sign, V(pm, 13 * x + 12, 13 * x + 13), V("ix", k, k + 1))
+                act(V("signs", 16 * k, 16 * k + 13), V(pm, 13 * x, 13 * x + 13), -1.0, F.Sign, V(pm, 13 * x + 12, 13 * x + 13), V("ix", k, k + 1))
             for x in range(2):
                 ts(V("hm", o + 169 * x, o + 169 * x + 169), V("we", 0, 169), V("ix", 2 * f + x, 2 * f + x + 1), A.is_gt)
-            scan(V("kr", o, o + 338), V("hm", o, o + 338), V("df"), 0.0, A.mult, A.add)
-            row = V("kr", o + 12, o + 338, 13)
+            scan(V("kr", o, o + 338), V("hm", o, o + 338), V("df", 1, 676, 2), 0.0, A.mult, A.add)
             if f == 0:
                 ts(V("pen", 0, 25), V("kr", 25, 338, 13), 0.0, A.not_equal, -BIG, A.mult)
                 tt(V("s2", 0, 25), scores, V("pen", 0, 25), A.add)
-            a, p0, s0, k0 = 52 * f, (0, 156)[f], (52, 208)[f], (104, 130)[f]
-            tt(V("ka", a, a + 26), V("k2c"), row, A.subtract)
-            tt(V("ka", a + 26, a + 52), V("k2c"), row, A.add)
-            scan(V("ps", k0, k0 + 26), V("hm", o + 156, o + 182), V("dk"), 0.0, A.mult, A.add)
-            scan(V("ps", p0, p0 + 52), V("rsk"), V("ka", a, a + 52), -BIG, A.min, A.max)
-            scan(V("ps", s0 + 1, s0 + 52), V("ka", a + 1, a + 52), V("ps", p0, p0 + 51), V("nq", 0, 1), A.max, A.min)
-            ts(V("di", 10 * f, 10 * f + 10), V("ps", 130 * f + 12, 130 * f + 130, 13), Q, A.mult)
-            ts(V("dj", 10 * f, 10 * f + 10), V("di", 10 * f, 10 * f + 10), 511, A.bitwise_and)
-            la, lb, lk = (0, 2)[f], (4, 6)[f], (8, 0)[f]
-            for b in range(4):
-                ts(V("gl", 40 * f + 10 * b, 40 * f + 10 * b + 10), V("dj", 10 * f, 10 * f + 10), 4.0, A.mult, float(b), A.add)
-            for b in range(4):
-                c, e = 40 * f + 10 * b, 384 * f + 3 * b
-                h = 256 * f + 64 * b
-                act(V("ga", h, h + 64), ind(V("fx"), V("gl", c + la, c + la + 4)))
-                for k in range(2):
-                    tt(V("sa", e + k, 384 * f + 384, 12), ind(V("fx"), V("gl", c + lb + 2 * k, c + lb + 2 * k + 2)), V("ga", h + 32 * k, h + 32 * k + 32), A.add)
-            for b in range(4):
-                c, e = 40 * f + 10 * b, 384 * f + 3 * b
-                act(V("sb", e + 1, 384 * f + 384, 12), ind(V("fx"), V("gl", c + lk, c + lk + 2)), 2.0)
-            scan(V("sy", 384 * f, 384 * f + 384), V("sa", 384 * f, 384 * f + 384), V("sb", 384 * f, 384 * f + 384), -BIG, A.max, A.subtract)
-            ts(V("yt", 128 * f, 128 * f + 128), V("sy", 384 * f + 1, 384 * f + 384, 3), 0.5, A.mult)
+            scan(V("ps", 208 + 26 * f, 234 + 26 * f), V("hm", o + 156, o + 182), V("dk"), 0.0, A.mult, A.add)
+        rows = V("kr", 12, 676, 13)
+        tt(V("ka", 0, 52), V("k2c"), rows, A.subtract)
+        tt(V("ka", 52, 104), V("k2c"), rows, A.add)
+        scan(V("ps", 0, 104), V("rsk"), V("ka"), -BIG, A.min, A.max)
+        scan(V("ps", 105, 208), V("ka", 1, 104), V("ps", 0, 103), 384.0 / Q, A.max, A.min)
+        ts(V("di"), V("ps", 12, 208, 13), Q, A.mult)
+        ts(V("dj"), V("di"), 511, A.bitwise_and)
+        for b in range(4):
+            ts(V("gl", 16 * b, 16 * b + 16), V("dj"), 4.0, A.mult, float(b), A.add)
+            ts(V("so", 4 * b, 4 * b + 4), V("ps", 220, 260, 13), 4.0 * Q, A.mult, float(b), A.add)
+        for b in range(4):
+            act(V("sb", 3 * b + 1, 768, 12), ind(V("fx"), V("so", 4 * b, 4 * b + 4)), 2.0)
+            act(V("ga", 128 * b, 128 * b + 128), ind(V("fx"), V("gl", 16 * b, 16 * b + 8)))
+            for k in range(2):
+                h = 128 * b + 64 * k
+                tt(V("sa", 3 * b + k, 768, 12), ind(V("fx"), V("gl", 16 * b + 8 + 4 * k, 16 * b + 12 + 4 * k)), V("ga", h, h + 64), A.add)
+        scan(V("sy"), V("sa"), V("sb"), -BIG, A.max, A.subtract)
+        ts(V("yt", 0, 256), V("sy", 1, 768, 3), 0.5, A.mult)
         quant(V("yc%d" % t), V("yp%d" % t), V("yt"))
         src, dst, ca, cb = route(T, topo, rank)
         sent = post([(dst, out, 64 + 128 * t, mine + str(t), sem + str(t)) if k is None else (k, mid + str(t), 0, mine + str(t), sem + str(t))
@@ -441,19 +578,18 @@ def rank_program(g, core, T, topo):
             for k in range(R + 1):
                 dma("y", u8(T, "lc", 128 * k, 128 * k + 64), u8(T, "zq", 0, 64), V("zq")[1], V("lc", 128 * k, 128 * k + 64)[1])
                 dma("y", u8(T, "lp", 128 * k, 128 * k + 64), u8(T, "zs", 0, 64), V("zs")[1], V("lp", 128 * k, 128 * k + 64)[1])
-        rows = V("kr", 12, 676, 13)
-        ts(V("oo"), rows, MU, A.is_equal, -2.0, A.mult)
-        act(V("pp"), rows, 1.0, F.Relu)
-        act(V("nn"), rows, -1.0, F.Relu)
-        tt(V("w", 104, 130), V("kr", 12, 338, 13), V("kr", 350, 676, 13), A.add)
-        tt(V("w", 0, 52), V("pp"), V("oo"), A.add)
-        tt(V("w", 52, 104), V("nn"), V("oo"), A.add)
-        act(V("sta"), ind(V("w"), V("La")), 64.0, bias=192.0)
-        act(V("stb"), ind(V("w"), V("Lb")), 1.0 / 64)
+        ts(V("oo", 0, 52), rows, MU, A.is_equal, -2.0, A.mult)
+        act(V("oo", 52, 104), V("oo", 0, 52))
+        act(V("oo", 104, 130), V("kr", 12, 338, 13))
+        act(V("pp", 0, 52), rows, 1.0, F.Relu)
+        act(V("pp", 52, 104), rows, -1.0, F.Relu)
+        act(V("pp", 0, 104), V("pp", 0, 104), bias=-16.0)
+        act(V("pp", 104, 130), V("kr", 350, 676, 13), bias=-16.0)
+        scan(V("w", 0, 130), V("oo"), V("pp"), -BIG, A.max, A.add)
+        act(V("sta"), ind(V("w"), V("La")), 64.0, bias=1216.0)
+        act(V("stb"), ind(V("w"), V("Lb")), 1.0 / 64, bias=0.25)
         for b in range(4):
             act(V("y32", 64 * b, 64 * b + 64), V("yt", b, 256, 4), 32.0)
-        for b in range(4):
-            ts(V("so", 4 * b, 4 * b + 4), V("dj", 8, 12), 4.0, A.mult, float(b), A.add)
         for d in range(1, 7):
             scan(V("pr", 120 * d - 120, 120 * d), V("sta", 0, 120), V("stb", 10 * d, 10 * d + 120), -BIG, A.max, A.mult)
         scan(V("s5"), V("sg"), V("pr"), 0.0, A.mult, A.add)
@@ -465,9 +601,11 @@ def rank_program(g, core, T, topo):
             table()
         else:
             act(V("win", 288, 289), V("win", 289, 290))
-            act(V("tb"), ind(V("win"), V("LT")))
-            for e in range(12):
-                act(V("ob", e, 300, 12), V("tb", 14 + e, 338, 13), -1.0)
+            act(V("tb", 0, 352), ind(V("win"), V("LT")))
+            ts(V("lo"), V("lm", 0, 20), 1.0 / 12, A.mult, -5.5 / 12, A.add)
+            tt(V("lI", 0, 20), V("lo"), V("lm", 0, 20), A.add)
+            ts(V("LO"), V("lI", 0, 20), 14.0, A.add, 351.0, A.min)
+            act(V("ob"), ind(V("tb", 0, 352), V("LO", 0, 19)), -1.0)
             for x in range(2):
                 dma("y", T.oa[:, 144 * x:144 * x + 144], T.ob[:, 156 * x:156 * x + 144], V("ob")[1], [])
             quant(V("vq"), V("vs"), V("vt0"))
@@ -479,11 +617,14 @@ def rank_program(g, core, T, topo):
                 out, b = T.psE[:, 512 * h:512 * h + 128], 256 * h
                 e.matmul_mx(out, T.wq[:, b:b + 128], T.wp[:, b:b + 128], T.lc[:, o + 64:o + 192], T.lp[:, o + 64:o + 192], True, False)
                 return e.matmul_mx(out, T.wq[:, b + 128:b + 256], T.wp[:, b + 128:b + 256], T.lc[:, o:o + 128], T.lp[:, o:o + 128], False, True)
-            run("t", pair, [V("wq"), V("wp"), V("lc"), V("lp")], [V("psE", 512 * h, 512 * h + 128)], 370.0, (sent, arr, NEAR if direct == (t % 2 == 0) else FAR))
+            run("t", pair, [V("wq"), V("wp"), V("lc"), V("lp")], [V("psE", 512 * h, 512 * h + 128)], 420.0, (sent, arr))
         for h in range(2):
             tt(V("v32", 128 * h, 128 * h + 128), V("psE", 512 * h, 512 * h + 128), V("y32", 128 * h, 128 * h + 128), A.add)
-            ts(V("vt", 128 * h, 128 * h + 128), V("v32", 128 * h, 128 * h + 128), 0.03125, A.mult)
-        run("v", lambda e: e.tensor_copy(T.fx[:, 0:1664].indirect(T.so[:, 0:16]), T.vt[:]), [V("vt"), V("so")], [V("fx")], 1060.0)
+            if h:
+                act(V("vt", 128, 256), V("v32", 128, 256), 0.03125)
+            else:
+                ts(V("vt", 0, 128), V("v32", 0, 128), 0.03125, A.mult)
+            scatter(V("fx"), V("so", 8 * h, 8 * h + 8), V("vt", 128 * h, 128 * h + 128))
         if t < R - 1:
             iota(V("fx", 1536, 1664), [[0, 128]])
 
@@ -495,6 +636,8 @@ def rank_program(g, core, T, topo):
         dma("sys"[k], T.y[:, a:a + 128], T.ysb[:, a:a + 128], V("ysb", a, a + 128)[1], [])
     for k in range(4):
         dma("ys"[k % 2], T.osc[4 * k:4 * k + 4, :], T.xs[32 * k:32 * k + 4, :], V("xs")[1], [], 2000.0)
+    if not go:
+        return ops
     issue()
     for sem in count:
         need("g", sem, count[sem], {})

from concourse.mybir import dt, AluOpType, ActivationFunctionType

N, C, R = 8, 384, 3
BIG = 2.0 ** 90
NONE = 2.0 ** 79
Q = 16384.0
MU = 1.0 / 64
SHIFT = 192.0
CASES = ((50.0, 180.0, 25.0, (1100.0, 2400.0), (800.0, 1600.0), 0.7, 1.0), (50.0, 60.0, 20.0, (1900.0, 4000.0), (400.0, 800.0), 1.0, 1.0))
PLAN, TRIES = {}, 32000
SCRATCH, CODES = {}, set()


def declare(dtype, spec):
    for item in spec.split():
        name, cols = item.split(":")
        where = "psum" if name in ("psP", "psE") else "sbuf"
        SCRATCH[name] = (where, [128, int(cols)], dtype)
        if dtype == "float8_e4m3fn_x4":
            CODES.add(name)


declare("bfloat16", "fx:1664 ut:512 vt0:512 yt:512 zt:512 et:520 ones:128 ga:512 sa:768 sb:768 sy:768 y32:256 v32:256 vt:256 "
        "hm:676 we:170 tb:704 df:676 alt:338 kr:676 win:304 bs:144 sp:144 pr:720 s5:720 sg:720 sta:128 stb:192 w:192 pp:130 oo:130 "
        "iC:400 cap:400 rs2:400 rsk:104")
declare("float8_e4m3fn_x4", "uq:128 urq:128 vq:128 eq:512 zq:128 wq:512 xq:384 lc:448 " + " ".join("yc%d:128 rc%d:64" % (t, t) for t in range(R)))
declare("uint8", "us:128 urs:128 vs:128 es:512 zs:128 wp:512 xs:384 lp:448 " + " ".join("yp%d:128 rp%d:64" % (t, t) for t in range(R)))
declare("float32", "psP:1536 psE:2048 psc:416 gm:400 sc:400 pm1:26 pm2:26 pen:26 s2:26 rs25:26 ix:4 signs:64 ka:104 ps:260 "
        "k2i:26 k2c:52 nlf:28 nq:28 dk:26 ob:304 ysb:384 rt:384 iK:384 pf:4 pd:4 few:504")
PART = {}
for item in "lm:22 lA:22 lB:22 lC:22 lD:22 lE:22 lF:22 lG:22 lH:22 lI:22 uA:9 uB:9 uC:9 uD:9 uE:9 mA:12 mB:12 mC:12 mD:24 mE:12 mF:12".split():
    PART[item[:2]] = (24 * len(PART), int(item[3:]))
declare("int32", "di:16 dj:16 lo:20 ndi:24 ari:296 pI:4 pA:4 ui:8 li:22 mi:12 mj:24")
declare("uint16", "gl:80 LP:10 LO:20 so:16 nd16:24 nl:26 ul:8 LT:22 L0:22 La:8 Lb:12")
DMAS = 34
SEMAPHORES = ["qv", "qs", "qt", "qg", "sent"] + ["d%d" % i for i in range(DMAS)] + ["ac%d" % t for t in range(R)] + ["ap%d" % t for t in range(R)]


def route(T, topo, r):
    src, dst = T.cores[r], T.cores[(r + 1) % N]
    if topo.may_write(src, dst):
        return src, dst, None, None
    c = [k for k in topo.cores_of(src) if k not in T.cores and topo.may_write(k, dst)]
    c.sort(key=lambda k: (topo.die(k) != topo.die(src), k))
    return src, dst, c[0], c[1 % len(c)]


def u8(T, name, a, b):
    v = T[name][:, a:b]
    return v.bitcast(dt.uint8) if name in CODES else v


def send(g, T, topo, core, to, out, at, src, sem):
    rid, pid = topo.addr(to, core)
    g.remote_dma(u8(T, out, at, at + 64), u8(T, src, 0, 64), T.sem[sem], T.sem.sent, pid, rid, topo.mask(core, to))
    return len(topo.engines(core, to))


def relay_program(g, core, T, topo):
    total = 0
    for t in range(R):
        for r in range(N):
            src, dst, ca, cb = route(T, topo, r)
            for k, sem, mid, out in ((ca, "ac%d" % t, "rc%d" % t, "lc"), (cb, "ap%d" % t, "rp%d" % t, "lp")):
                if k == core:
                    g.wait_ge(T.sem[sem], len(topo.engines(src, core)))
                    total += send(g, T, topo, core, dst, out, 64 + 128 * t, mid, sem)
    if total:
        g.wait_ge(T.sem.sent, total)


def plan(first, second):
    n, ops = len(first), first + second
    m = len(ops)
    names = {}
    line = [names.setdefault((ops[k][0], k < n), len(names)) for k in range(m)]
    marks = [k for k in range(m) if ops[k][3] == "sent"]
    graphs = []
    for wake, across, more, way, once, by, speed in CASES:
        cost = [o[2] * by if o[4] == 16 else o[2] * speed + more for o in ops]
        busy = [90.0 if ops[k][4] == 16 else cost[k] for k in range(m)]
        before = [[] for _ in range(m)]
        for k in range(m):
            side = int(k >= n)
            before[k] += [(side * n + d, busy[side * n + d]) for d in ops[k][7]]
            for d in ops[k][5]:
                d += side * n
                before[k].append((d, cost[d] + (0.0 if d in marks else wake if ops[d][0] == ops[k][0] and ops[d][4] == 1 else across)))
                if ops[k][6] and d in marks:
                    t = marks.index(d) % R
                    before[k].append((marks[t + R * (1 - side)], way[side] + (0.0 if t else once[side])))
        graphs.append((cost, busy, before))
    cost, busy, before = graphs[0]
    behind = [[] for _ in range(m)]
    for k in range(m):
        for d, c in before[k]:
            behind[d].append((k, c))
    tails = [k for k in range(m) if not behind[k]]

    def times(order, a=0, seen=None):
        value, out, who0 = 0.0, [], [-1] * len(names)
        for k in order[:a]:
            who0[line[k]] = k
        rest = order[a:]
        for i, (cost, busy, before) in enumerate(graphs):
            start, ahead = (list(seen[i][0]), list(seen[i][1])) if seen else ([0.0] * m, [-1] * m)
            who = list(who0)
            end = [start[k] + busy[k] if k >= 0 else 0.0 for k in who]
            for k in rest:
                q = line[k]
                t = end[q]
                for d, c in before[k]:
                    x = start[d] + c
                    if x > t:
                        t = x
                start[k], end[q], ahead[k], who[q] = t, t + busy[k], who[q], k
            value += max(start[k] + cost[k] for k in tails) + 0.01 * sum(start[k] for k in marks)
            out.append((start, ahead))
        return value / len(graphs), out

    left, back = [len(e) for e in behind], list(tails)
    for k in back:
        for d, c in before[k]:
            left[d] -= 1
            if not left[d]:
                back.append(d)
    far = [0.0] * m
    for k in back:
        far[k] = max([far[u] + c for u, c in behind[k]] + [cost[k]])
    start, taken = [0.0] * m, [[] for _ in names]
    for k in sorted(range(m), key=lambda k: -far[k]):
        t0, at = max([start[d] + c for d, c in before[k]] or [0.0]), 0
        for a, b in taken[line[k]]:
            if t0 + busy[k] <= a:
                break
            t0, at = max(t0, b), at + 1
        taken[line[k]].insert(at, (t0, t0 + busy[k]))
        start[k] = t0
    order = sorted(range(m), key=lambda k: (start[k], -far[k]))
    value, seen = times(order)
    best, seed = (value, order), [20261]

    def draw(count):
        seed[0] = (seed[0] * 1103515245 + 12345) % 2147483648
        return (seed[0] >> 8) % count

    where = [0] * m
    for i, u in enumerate(order):
        where[u] = i
    for trial in range(TRIES):
        case = draw(len(graphs))
        (cost, busy, before), (start, ahead) = graphs[case], seen[case]
        k = marks[draw(len(marks))] if draw(10) < 3 else max(tails, key=lambda k: start[k] + cost[k])
        held = []
        while start[k] > 0.0:
            d, x = -1, -1.0
            for e, c in before[k]:
                if start[e] + c > x:
                    d, x = e, start[e] + c
            if x < start[k] - 0.01:
                held.append((k, ahead[k]))
                k = ahead[k]
            else:
                if ahead[k] >= 0 and draw(10) == 0:
                    held.append((k, ahead[k]))
                k = d
        if not held:
            continue
        k, j = held[draw(len(held))]
        if draw(2):
            for _ in range((0, 0, 1, 2, 4, 8, 20)[draw(7)]):
                if ahead[j] >= 0:
                    j = ahead[j]
            move, todo, a, b = {k}, [k], where[j], where[k] + 1
            while todo:
                for d, c in before[todo.pop()]:
                    if where[d] >= a and d not in move:
                        move.add(d)
                        todo.append(d)
            if j in move:
                continue
            new = order[:a] + [u for u in order[a:b] if u in move] + [u for u in order[a:b] if u not in move] + order[b:]
        else:
            move, todo, a, b = {j}, [j], where[j], min(m, where[k] + 1 + (0, 0, 5, 20, 60, 150)[draw(6)])
            while todo:
                for u, c in behind[todo.pop()]:
                    if where[u] < b and u not in move:
                        move.add(u)
                        todo.append(u)
            new = order[:a] + [u for u in order[a:b] if u not in move] + [u for u in order[a:b] if u in move] + order[b:]
        v, s = times(new, a, seen)
        if v <= value + 0.2 * draw(1000) * (1.0 - trial / TRIES) ** 2:
            order, value, seen = sorted(new, key=lambda k: s[0][0][k]), v, s
            for i, u in enumerate(order):
                where[u] = i
            if v < best[0]:
                best = (v, new)
    return [k for k in best[1] if k < n], [k - n for k in best[1] if k >= n]


def overlap(a, b):
    if a[0] != b[0] or a[1] >= b[2] or b[1] >= a[2]:
        return False
    return not (a[3] == b[3] > 1 and (a[1] - b[1]) % a[3])


def rank_program(g, core, T, topo):
    rank = T.rank_of(core)
    if rank is None:
        relay_program(g, core, T, topo)
        return
    if not PLAN:
        PLAN[True], PLAN[False] = plan(calls(g, core, T, topo, True, False), calls(g, core, T, topo, False, False))
    calls(g, core, T, topo, route(T, topo, (rank - 1) % N)[2] is None, True)


def calls(g, core, T, topo, direct, go):
    rank = T.rank_of(core)
    A = AluOpType
    F = ActivationFunctionType
    queue = {"v": g.vector, "s": g.scalar, "t": g.tensor, "g": g, "y": g.sync}
    count = {}
    known = {k: {} for k in queue}
    free = ["d%d" % i for i in range(DMAS)]
    ops, last = [], {}

    def add(q, call, reads, writes, cost, sem=None, inc=1, after=(), arrivals=()):
        k = len(ops)
        deps = set(after)
        for kind, regions in (("r", reads), ("w", writes)):
            for x in regions:
                for o, y, d in last.get(x[0], []):
                    if (kind == "w" or o == "w" or x[0] in ("psP", "psE") and ops[d][0] != q) and overlap(x, y):
                        deps.add(d)
        for x in writes:
            last[x[0]] = [e for e in last.get(x[0], []) if not (e[1][1] >= x[1] and e[1][2] <= x[2] and x[3] == 1)]
        for kind, regions in (("r", reads), ("w", writes)):
            for x in regions:
                last.setdefault(x[0], []).append((kind, x, k))
        ops.append((q, call, cost, sem or "q" + q, inc, sorted(deps), arrivals, []))
        return k

    def run(q, call, reads, writes, cost, arr=None):
        bank = lambda x: (x[0], x[1] // 512 * 512, x[1] // 512 * 512 + 512, 1) if x[0] in ("psP", "psE") else x
        reads = [bank(x) for o in reads for x in o[1]]
        writes = [bank(x) for o in writes for x in o[1]]
        add(q, lambda e: call(e).then_inc(T.sem["q" + q], 1), reads, writes, cost, after=[arr[0]] if arr else (), arrivals=arr[1] if arr else ())

    def dma(q, out, in_, reads, writes, cost=2400.0, after=()):
        sem = free.pop(0)
        add(q, lambda e: e.dma_start(out, in_).then_inc(T.sem[sem], 16), reads, writes, cost, sem, 16, after)

    def post(writes):
        def call(e):
            for to, out, at, mine, sem in writes:
                count["sent"] = count.get("sent", 0) + send(e, T, topo, core, to, out, at, mine, sem)
        return add("g", call, [(w[3], 0, 128, 1) for w in writes], [], 600.0, "sent", 0)

    def issue():
        mark = [None] * len(ops)
        for k in PLAN[direct]:
            q, call, cost, sem, inc, deps, arrivals = ops[k][:7]
            for d in sorted(deps, key=lambda d: -mark[d][1]):
                if mark[d][0] != "sent":
                    need(q, *mark[d])
            for a, v in arrivals:
                need(q, a, v, {})
                count[a] = v
            call(queue[q])
            if inc:
                count[sem] = count.get(sem, 0) + inc
            mark[k] = (sem, count.get(sem, 0), dict(known[q]))

    def need(q, sem, val, clock):
        if known[q].get(sem, 0) < val:
            queue[q].wait_ge(T.sem[sem], val)
            known[q][sem] = val
            for s in clock:
                known[q][s] = max(known[q].get(s, 0), clock[s])

    def V(name, a=0, b=None, step=1):
        if name in PART:
            name, a, b = "few", PART[name][0] + a, PART[name][0] + (PART[name][1] if b is None else b)
        b = SCRATCH[name][1][1] if b is None else b
        return (T[name][:, a:b:step] if step > 1 else T[name][:, a:b], [(name, a, b, step)])

    def ind(win, off):
        return (win[0].indirect(off[0]), win[1] + off[1], True)

    def val(s):
        return s[0] if isinstance(s, tuple) else s

    def reg(*ss):
        return [s for s in ss if isinstance(s, tuple)]

    def size(v):
        name, a, b, step = v[1][0]
        return (b - a + step - 1) // step

    def fast(out, *v):
        if len(v[0]) > 2:
            return 50 + 1.62 * size(out)
        return max(66, 1.04 * size(out) * (0.5 if all(SCRATCH[x[1][0][0]][2] in ("bfloat16", "uint16") for x in v + (out,)) else 1))

    def tt(out, a, b, op):
        n = size(out)
        cost = 50 + 1.62 * n if len(a) > 2 else max(66, 1.04 * (n if a[1][0][0] in ("psP", "psE") else 2 * n))
        run("v", lambda e: e.tensor_tensor(out[0], a[0], b[0], op), [a, b], [out], cost)

    def ts(out, a, s1, op0, s2=None, op1=None):
        if op1 is None:
            run("v", lambda e: e.tensor_scalar(out[0], a[0], val(s1), None, op0), [a] + reg(s1), [out], fast(out, a))
        else:
            run("v", lambda e: e.tensor_scalar(out[0], a[0], val(s1), val(s2), op0, op1), [a] + reg(s1, s2), [out], fast(out, a))

    def cp(out, a):
        run("v", lambda e: e.tensor_copy(out[0], a[0]), [a], [out], fast(out, a))

    def scatter(win, off, a):
        run("v", lambda e: e.tensor_copy(win[0].indirect(off[0]), a[0]), [a, off], [win], 50 + 3.94 * size(a))

    def scan(out, d0, d1, initial, op0, op1):
        run("v", lambda e: e.tensor_tensor_scan(out[0], d0[0], d1[0], initial, op0, op1), [d0, d1], [out], fast(out, d0, d1))

    def fill(out, c):
        run("v", lambda e: e.memset(out[0], c), [], [out], fast(out, out))

    def quant(q, s, t):
        run("v", lambda e: e.quantize_mx(q[0], s[0], t[0]), [t], [q, s], 15 + 0.275 * size(t))

    def mm(out, w, ws, x, xs):
        run("t", lambda e: e.matmul_mx(out[0], w[0], ws[0], x[0], xs[0], True, True), [w, ws, x, xs], [out], 1.4 * size(x) + 23)

    def act(out, a, scale=1.0, func=None, bias=None, accum=None):
        kw = {}
        if scale != 1.0:
            kw["scale"] = scale
        if bias is not None:
            kw["bias"] = val(bias)
            func = func or F.Identity
        if accum is not None:
            kw["accum_out"] = accum[0]
        run("s", lambda e: e.activation(out[0], a[0], func or F.Copy, **kw), [a] + reg(bias), [out] + reg(accum),
            65 + 1.62 * size(out) if len(a) > 2 else max(66, 1.04 * size(out)) + (20 if accum is not None else 0))

    def iota(out, pattern, base=0, cm=0):
        cost = 130 + 2.1 * (out[1][0][2] - out[1][0][1])
        if SCRATCH[out[1][0][0]][2] == "int32":
            run("g", lambda e: e.iota(out[0], pattern, base, cm), [], [out], cost)
        else:
            run("g", lambda e: e.iota(out[0], pattern, base, cm, allow_small_or_imprecise_dtypes=True), [], [out], cost)

    dma("y", T.ndi[:], T.nd[:], [], V("ndi")[1], 2100.0)
    dma("s", T.ut[:], T.u[:], [], V("ut")[1], 2800.0)
    for k, q in enumerate("ysy"):
        dma(q, T.fx[:, 512 * k:512 * k + 512], T.x[:, 512 * k:512 * k + 512], [], V("fx", 512 * k, 512 * k + 512)[1], 2900.0 + 300 * k)
    dma("s", T.ari[:, 0:288], T.ar[:], [], V("ari", 0, 288)[1], 3300.0)
    for a, b in ((0, 2), (2, 4), (1, 3), (3, 5)):
        ops[b][7].append(a)

    iota(V("pI"), [[0, 4]], 0, 1)
    iota(V("lm"), [[16, 22]])
    iota(V("iK"), [[1, 384]])
    iota(V("ui"), [[16, 8]])
    iota(V("ari", 288, 296), [[0, 8]])
    fill(V("ones"), 1.0)
    one = lambda n: V("ones", 0, n)
    for k in range(0, 520, 104):
        act(V("et", k, k + 104), one(104), 0.0)
    run("g", lambda e: e.affine_select(T.et[:, 3:515:4], T.ones[:], [[-1, 128]], A.is_equal, 0.0, 0, 1), [V("ones")], [V("et")], 900.0)
    iota(V("iC"), [[0, 25], [1, 16]])
    iota(V("uA"), [[0, 3], [8, 3]])
    iota(V("uB"), [[2, 3], [0, 3]], 1)
    iota(V("alt"), [[0, 169], [1, 2]])
    iota(V("we", 0, 169), [[0, 13], [1, 13]])
    iota(V("k2i"), [[0, 2], [-512, 13]], int(512 * 13 - Q))
    iota(V("win", 288, 304), [[0, 16]])
    fill(V("rs2"), 0.0)
    iota(V("fx", 1536, 1664), [[0, 128]])
    iota(V("w"), [[0, 192]], -16)
    iota(V("sg", 0, 720, 5), [[0, 144]])
    iota(V("sg", 3, 720, 5), [[0, 144]], -1)
    for k in (1, 2, 4):
        fill(V("sg", k, 720, 5), 1.0)
    fill(V("zt"), 0.0)
    fill(V("yt", 256, 512), 0.0)
    fill(V("sb", 0, 768, 3), 0.0)
    early = [k for k in range(len(ops)) if ops[k][0] == "g"]
    for a, b in zip(early, early[1:]):
        ops[b][7].append(a)
    act(V("win", 288, 289), one(1), MU)
    act(V("psc", 384, 416), one(32), -BIG)
    for h in range(2):
        act(V("sa", 2 + 384 * h, 384 + 384 * h, 3), one(128), -BIG)
        act(V("sb", 2 + 384 * h, 384 + 384 * h, 3), one(128), BIG)
    act(V("rs25"), one(26), BIG)
    act(V("rs25", 12, 13), one(1), -NONE)
    act(V("rsk"), one(104), BIG)
    act(V("rsk", 0, 104, 13), one(8), -BIG)
    for n in ("pm1", "pm2"):
        act(V(n, 0, 1), one(1), -NONE)
    act(V("k2i"), V("k2i"), 1.0 / Q)

    ts(V("pA", 0, 1), V("pI", 0, 1), 15, A.bitwise_and)
    ts(V("pA", 1, 2), V("pI", 1, 2), 1, A.logical_shift_right, 7, A.bitwise_and)
    ts(V("pA", 2, 3), V("pI", 2, 3), 1, A.bitwise_and)
    cp(V("pf", 0, 3), V("pA", 0, 3))
    p16, p8, p1 = (V("pf", k, k + 1) for k in range(3))
    for k, c in ((0, 384.0), (13, 400.0)):
        act(V("nlf", k, k + 1), p16, bias=c)
    act(V("nlf", 26, 28), one(2), 0.0)
    beside = [len(ops) - 3, len(ops) - 2, len(ops) - 1]
    act(V("pd", 0, 1), p1, 144.0)

    def score_products(w, ws):
        for k in range(3):
            a = 128 * k
            quant(V("xq", a, a + 128), V("xs", a, a + 128), V("fx", 4 * a, 4 * a + 512))
            mm(V("psP", 512 * k, 512 * k + 128), w, ws, V("xq", a, a + 128), V("xs", a, a + 128))

    def unpack_products():
        for b in range(4):
            mm(V("psE", 512 * b, 512 * b + 384), V("eq", 128 * b, 128 * b + 128), V("es", 128 * b, 128 * b + 128), V("xq"), V("xs"))

    cp(V("nd16"), V("ndi"))
    act(V("rt", 0, 192), ind(V("iK"), V("nd16", 0, 12)))
    cp(V("rt", 192, 384), ind(V("iK"), V("nd16", 12, 24)))
    for x in range(2):
        dma("y", T.nlf[:, 13 * x + 1:13 * x + 13], T.rt[0:128:16, 192 * x:192 * x + 192], V("rt", 192 * x, 192 * x + 192)[1],
            [("nlf", 13 * x + 1, 13 * x + 13, 1)], 2100.0, beside)
    dma("y", T.wq[:, 0:512].bitcast(dt.uint8), T.wc[:], V("nlf")[1], V("wq")[1], 4000.0)
    dma("y", T.wp[:], T.ws[:], V("nlf")[1], V("wp")[1])
    dma("y", T.vt0[:], T.v[:], V("nlf")[1], V("vt0")[1])
    ts(V("cap"), V("iC"), p16, A.not_equal, -BIG, A.mult)
    act(V("cap", 192, 208), one(16), -BIG)
    cp(V("ul"), V("ui"))
    act(V("rs2", 0, 400, 16), one(25), -BIG)
    quant(V("uq"), V("us"), V("ut"))
    run("v", lambda e: e.tensor_copy(T.urq[:, 0:128].bitcast(dt.uint32), T.uq[:, 0:128].bitcast(dt.uint32).indirect(T.ul[:, 0:8])),
        [V("uq"), V("ul")], [V("urq")], 260.0)
    act(V("urs"), ind(V("us"), V("ul")))
    for b in range(4):
        quant(V("eq", 128 * b, 128 * b + 128), V("es", 128 * b, 128 * b + 128), V("et", 3 - b, 515 - b))
    cp(V("nl", 0, 25), V("nlf", 1, 26))
    act(V("nq"), V("nlf"), 1.0 / Q)
    tt(V("k2c", 0, 26), V("nq", 0, 26), V("k2i"), A.add)
    act(V("k2c", 0, 26, 13), one(2), 384.0 / Q)
    act(V("k2c", 26, 52), V("k2c", 0, 26))
    tt(V("dk"), V("nq", 0, 26), V("nq", 1, 27), A.subtract)
    act(V("dk", 12, 13), V("nq", 12, 13))

    ts(V("uA"), V("uA"), p8, A.add)
    ts(V("uC"), V("uA"), 12.0, A.is_ge)
    ts(V("uD"), V("uA"), 12.0, A.is_ge, -12.0, A.mult)
    tt(V("uB"), V("uB"), V("uC"), A.add)
    tt(V("uA"), V("uA"), V("uD"), A.add)
    tt(V("uB"), V("uB"), V("uA"), A.add)
    ts(V("uE"), V("uA"), 12.0, A.mult, V("pd", 0, 1), A.add)
    ts(V("uC"), V("uB"), 12.0, A.is_ge, -12.0, A.mult)
    tt(V("uE"), V("uE"), V("uB"), A.add)
    tt(V("uE"), V("uE"), V("uC"), A.add)
    cp(V("LP", 0, 9), V("uE"))
    act(V("bs"), ind(V("ari"), V("LP", 0, 9)), bias=-SHIFT)

    ts(V("lm"), V("lm"), p16, A.add)
    ts(V("li"), V("lm"), 1.0 / 13, A.mult, -6.0 / 13, A.add)
    ts(V("lB"), V("lm"), 169.0, A.is_ge)
    ts(V("lC"), V("lm"), 169.0, A.is_ge, -13.0, A.mult)
    ts(V("lD"), V("li"), -13.0, A.mult)
    tt(V("lA"), V("li"), V("lC"), A.add)
    tt(V("lD"), V("lD"), V("lm"), A.add)
    tt(V("lH"), V("lA"), V("lD"), A.mult)
    ts(V("lI"), V("lD"), 12.0, A.mult, -13.0, A.add)
    ts(V("lE"), V("lm"), 169.0, A.is_ge, 144.0, A.mult)
    ts(V("lH"), V("lH"), 0.0, A.is_equal, 289.0, A.mult)
    tt(V("lI"), V("lI"), V("lA"), A.add)
    tt(V("lI"), V("lI"), V("lE"), A.add)
    tt(V("lI"), V("lI"), V("lH"), A.max)
    ts(V("L0"), V("lI"), 289.0, A.min)
    tt(V("lC"), V("lA"), V("lD"), A.subtract)
    ts(V("lE"), V("lC"), 0.0, A.is_lt, 12.0, A.mult)
    act(V("lD"), V("lD"), 2.0, bias=-26.0)
    act(V("lA"), V("lA"), 2.0, bias=406.0)
    tt(V("lC"), V("lC"), V("lE"), A.add)
    act(V("lE"), V("lC"), 24.0)
    act(V("lF"), V("lC"), 1000.0, F.Relu, -6000.0)
    act(V("lG"), V("lC"), -288.0, F.Relu, 288.0)
    tt(V("lD"), V("lD"), V("lE"), A.add)
    tt(V("lA"), V("lA"), V("lE"), A.subtract)
    tt(V("lD"), V("lD"), V("lF"), A.add)
    tt(V("lG"), V("lG"), V("lH"), A.max)
    tt(V("lD"), V("lD"), V("lA"), A.min)
    tt(V("lD"), V("lD"), V("lB"), A.add)
    tt(V("lD"), V("lD"), V("lG"), A.max)
    ts(V("LT"), V("lD"), 289.0, A.min)

    def table(first=False):
        act(V("tb", 0, 704, 2), ind(V("ari"), V("L0")) if first else ind(V("win"), V("LT")))
        if first:
            for x in range(2):
                act(V("tb", 338 * x + 28, 338 * x + 338, 28), one(12), MU)
        for a in (0, 338):
            act(V("tb", a + 1, a + 338, 2), V("tb", a + 2, a + 340, 2), -1.0)
            scan(V("df", a, a + 338), V("alt"), V("tb", a, a + 338), 0.0, A.mult, A.add)

    def stream_lists():
        m = V("lm", 0, 12)
        ts(V("mi"), m, 0.2, A.mult, -0.4, A.add)
        cp(V("mA"), V("mi"))
        ts(V("mj", 0, 12), V("mi"), 1, A.bitwise_and)
        ts(V("mj", 12, 24), V("mi"), 1, A.logical_shift_right)
        act(V("mA"), V("mA"), -5.0)
        cp(V("mD"), V("mj"))
        tt(V("mA"), V("mA"), m, A.add)
        ts(V("mB"), V("mD", 12, 24), 12.0, A.is_ge, -12.0, A.mult)
        act(V("mC"), V("mD", 0, 12), 13.0, bias=105.0)
        act(V("mE"), V("mA"), -26.0)
        act(V("mF"), V("mA"), 1.0, F.Abs, -1.5)
        tt(V("mB"), V("mB"), V("mD", 12, 24), A.add)
        tt(V("mC"), V("mC"), V("mE"), A.add)
        ts(V("mF"), V("mF"), 1.0, A.is_lt, -104.0, A.mult)
        tt(V("mC"), V("mC"), V("mB"), A.add)
        cp(V("Lb"), V("mC"))
        tt(V("mF"), V("mF"), V("mC"), A.add)
        ts(V("La"), V("mF", 0, 8), 52.0, A.add)

    table(True)

    for t in range(R):
        score_products(V("urq"), V("urs"))
        unpack_products()
        for k in range(3):
            (cp if k else act)(V("psc", 128 * k, 128 * k + 128), V("psP", 512 * k, 512 * k + 128))
        for b in range(4):
            for h in range(2):
                act(V("fx", b + 768 * h, 768 * h + 768, 4), V("psE", 512 * b + 192 * h, 512 * b + 192 * h + 192))
        tt(V("gm"), ind(V("psc"), V("nl", 0, 25)), V("cap"), A.add)
        scan(V("sc"), V("rs2"), V("gm"), 0.0, A.add, A.max)
        scores = V("sc", 15, 400, 16)
        for f in range(2):
            pm, o = ("pm1", "pm2")[f], 338 * f
            scan(V(pm, 1, 26), V("rs25", 0, 25), V("s2", 0, 25) if f else scores, -NONE, A.min, A.max)
            for x in range(2):
                k = 2 * f + x
                act(V("signs", 16 * k, 16 * k + 13), V(pm, 13 * x, 13 * x + 13), -1.0, F.Sign, V(pm, 13 * x + 12, 13 * x + 13), V("ix", k, k + 1))
            for x in range(2):
                ts(V("hm", o + 169 * x, o + 169 * x + 169), V("we", 0, 169), V("ix", 2 * f + x, 2 * f + x + 1), A.is_gt)
            scan(V("kr", o, o + 338), V("hm", o, o + 338), V("df", 1, 676, 2), 0.0, A.mult, A.add)
            if f == 0:
                ts(V("pen", 0, 25), V("kr", 25, 338, 13), 0.0, A.not_equal, -BIG, A.mult)
                tt(V("s2", 0, 25), scores, V("pen", 0, 25), A.add)
            scan(V("ps", 208 + 26 * f, 234 + 26 * f), V("hm", o + 156, o + 182), V("dk"), 0.0, A.mult, A.add)
        rows = V("kr", 12, 676, 13)
        tt(V("ka", 0, 52), V("k2c"), rows, A.subtract)
        tt(V("ka", 52, 104), V("k2c"), rows, A.add)
        scan(V("ps", 0, 104), V("rsk"), V("ka"), -BIG, A.min, A.max)
        scan(V("ps", 105, 208), V("ka", 1, 104), V("ps", 0, 103), 384.0 / Q, A.max, A.min)
        ts(V("di"), V("ps", 12, 208, 13), Q, A.mult)
        ts(V("dj"), V("di"), 511, A.bitwise_and)
        for b in range(4):
            ts(V("gl", 16 * b, 16 * b + 16), V("dj"), 4.0, A.mult, float(b), A.add)
            ts(V("so", 4 * b, 4 * b + 4), V("ps", 220, 260, 13), 4.0 * Q, A.mult, float(b), A.add)
        for b in range(4):
            act(V("sb", 3 * b + 1, 768, 12), ind(V("fx"), V("so", 4 * b, 4 * b + 4)), 2.0)
            act(V("ga", 128 * b, 128 * b + 128), ind(V("fx"), V("gl", 16 * b, 16 * b + 8)))
            for k in range(2):
                h = 128 * b + 64 * k
                tt(V("sa", 3 * b + k, 768, 12), ind(V("fx"), V("gl", 16 * b + 8 + 4 * k, 16 * b + 12 + 4 * k)), V("ga", h, h + 64), A.add)
        scan(V("sy"), V("sa"), V("sb"), -BIG, A.max, A.subtract)
        ts(V("yt", 0, 256), V("sy", 1, 768, 3), 0.5, A.mult)
        quant(V("yc%d" % t), V("yp%d" % t), V("yt"))
        src, dst, ca, cb = route(T, topo, rank)
        sent = post([(dst, out, 64 + 128 * t, mine + str(t), sem + str(t)) if k is None else (k, mid + str(t), 0, mine + str(t), sem + str(t))
                     for k, sem, mid, out, mine in ((ca, "ac", "rc", "lc", "yc"), (cb, "ap", "rp", "lp", "yp"))])
        if t == 0:
            stream_lists()
            quant(V("zq"), V("zs"), V("zt"))
            for k in range(R + 1):
                dma("y", u8(T, "lc", 128 * k, 128 * k + 64), u8(T, "zq", 0, 64), V("zq")[1], V("lc", 128 * k, 128 * k + 64)[1])
                dma("y", u8(T, "lp", 128 * k, 128 * k + 64), u8(T, "zs", 0, 64), V("zs")[1], V("lp", 128 * k, 128 * k + 64)[1])
        ts(V("oo", 0, 52), rows, MU, A.is_equal, -2.0, A.mult)
        act(V("oo", 52, 104), V("oo", 0, 52))
        act(V("oo", 104, 130), V("kr", 12, 338, 13))
        act(V("pp", 0, 52), rows, 1.0, F.Relu)
        act(V("pp", 52, 104), rows, -1.0, F.Relu)
        act(V("pp", 0, 104), V("pp", 0, 104), bias=-16.0)
        act(V("pp", 104, 130), V("kr", 350, 676, 13), bias=-16.0)
        scan(V("w", 0, 130), V("oo"), V("pp"), -BIG, A.max, A.add)
        act(V("sta"), ind(V("w"), V("La")), 64.0, bias=1216.0)
        act(V("stb"), ind(V("w"), V("Lb")), 1.0 / 64, bias=0.25)
        for b in range(4):
            act(V("y32", 64 * b, 64 * b + 64), V("yt", b, 256, 4), 32.0)
        for d in range(1, 7):
            scan(V("pr", 120 * d - 120, 120 * d), V("sta", 0, 120), V("stb", 10 * d, 10 * d + 120), -BIG, A.max, A.mult)
        scan(V("s5"), V("sg"), V("pr"), 0.0, A.mult, A.add)
        scan(V("sp"), V("s5", 4, 720, 5), V("bs"), -BIG, A.max, A.add)
        ts(V("bs"), V("sp"), -SHIFT - 3.0, A.max, 3.0 - SHIFT, A.min)
        act(V("win", 0, 144), V("bs"), bias=SHIFT)
        act(V("win", 144, 288), V("bs"), -1.0, bias=-SHIFT)
        if t < R - 1:
            table()
        else:
            act(V("win", 288, 289), V("win", 289, 290))
            act(V("tb", 0, 352), ind(V("win"), V("LT")))
            ts(V("lo"), V("lm", 0, 20), 1.0 / 12, A.mult, -5.5 / 12, A.add)
            tt(V("lI", 0, 20), V("lo"), V("lm", 0, 20), A.add)
            ts(V("LO"), V("lI", 0, 20), 14.0, A.add, 351.0, A.min)
            act(V("ob"), ind(V("tb", 0, 352), V("LO", 0, 19)), -1.0)
            for x in range(2):
                dma("y", T.oa[:, 144 * x:144 * x + 144], T.ob[:, 156 * x:156 * x + 144], V("ob")[1], [])
            quant(V("vq"), V("vs"), V("vt0"))
        sender, arr = route(T, topo, (rank - 1) % N), []
        for sem, k in (("ac%d" % t, sender[2]), ("ap%d" % t, sender[3])):
            arr.append((sem, len(topo.engines(sender[0] if k is None else k, core))))
        for h in range(2):
            def pair(e, h=h, o=128 * t):
                out, b = T.psE[:, 512 * h:512 * h + 128], 256 * h
                e.matmul_mx(out, T.wq[:, b:b + 128], T.wp[:, b:b + 128], T.lc[:, o + 64:o + 192], T.lp[:, o + 64:o + 192], True, False)
                return e.matmul_mx(out, T.wq[:, b + 128:b + 256], T.wp[:, b + 128:b + 256], T.lc[:, o:o + 128], T.lp[:, o:o + 128], False, True)
            run("t", pair, [V("wq"), V("wp"), V("lc"), V("lp")], [V("psE", 512 * h, 512 * h + 128)], 420.0, (sent, arr))
        for h in range(2):
            tt(V("v32", 128 * h, 128 * h + 128), V("psE", 512 * h, 512 * h + 128), V("y32", 128 * h, 128 * h + 128), A.add)
            if h:
                act(V("vt", 128, 256), V("v32", 128, 256), 0.03125)
            else:
                ts(V("vt", 0, 128), V("v32", 0, 128), 0.03125, A.mult)
            scatter(V("fx"), V("so", 8 * h, 8 * h + 8), V("vt", 128 * h, 128 * h + 128))
        if t < R - 1:
            iota(V("fx", 1536, 1664), [[0, 128]])

    score_products(V("vq"), V("vs"))
    for k in range(3):
        a = 128 * k
        dma("y", T.oc[:, 4 * a:4 * a + 512], u8(T, "xq", a, a + 128), V("xq", a, a + 128)[1], [])
        (cp if k == 2 else act)(V("ysb", a, a + 128), V("psP", 512 * k, 512 * k + 128))
        dma("sys"[k], T.y[:, a:a + 128], T.ysb[:, a:a + 128], V("ysb", a, a + 128)[1], [])
    for k in range(4):
        dma("ys"[k % 2], T.osc[4 * k:4 * k + 4, :], T.xs[32 * k:32 * k + 4, :], V("xs")[1], [], 2000.0)
    if not go:
        return ops
    issue()
    for sem in count:
        need("g", sem, count[sem], {})
